import numpy as np
import ml_dtypes


def mxq(x, axis, fmt="e4m3"):
    dtype, down = {"e4m3": (ml_dtypes.float8_e4m3fn, 7), "e5m2": (ml_dtypes.float8_e5m2, 14)}[fmt]
    v = np.moveaxis(np.asarray(x, np.float32).astype(ml_dtypes.bfloat16).astype(np.float64), axis, -1)
    blocks = v.reshape(v.shape[:-1] + (-1, 32))
    amax = np.abs(blocks).max(-1, keepdims=True)
    byte = np.maximum(np.where(amax > 0, np.frexp(amax)[1] - 1 + 127, 0) - down, 1)
    scale = np.exp2(byte - 127.0)
    codes = (blocks / scale).astype(np.float32).astype(dtype).astype(np.float64)
    return np.moveaxis((codes * scale).reshape(v.shape), -1, axis)


WIDE = False


def mx_kscale(k):
    if not WIDE:
        return np.ones(k)
    levels = np.array([30, -30])
    if k % 512:
        return np.exp2(np.random.permutation(np.resize(levels, k // 32))).repeat(32)
    a = np.empty((k // 512, 16))
    for p in range(k // 512):
        a[p, :8] = np.random.permutation(np.resize(levels, 8))
        for g in range(8):
            far = levels[np.abs(levels - a[p, g]) >= 10]
            a[p, g + 8] = far[np.random.randint(len(far))]
    return np.exp2(a.ravel()).repeat(32)


def f64(x):
    return np.asarray(x).astype(np.float64)


def striped(idx):
    return np.tile(idx.reshape(-1, 16).T, (8, 1)).astype(np.uint16)


def unstriped(offs):
    return offs[:16].T.reshape(-1).astype(np.int64)


def bf(x):
    return np.asarray(x, np.float32).astype(ml_dtypes.bfloat16)


E2M1 = np.array([0.0, 0.5, 1.0, 1.5, 2.0, 3.0, 4.0, 6.0, -0.0, -0.5, -1.0, -1.5, -2.0, -3.0, -4.0, -6.0])


def pack_weight(w, fmt):
    k, n = w.shape
    w = f64(bf(w)).reshape(k // 32, 32, n)
    amax = np.abs(w).max(1)
    if fmt in ("e4m3", "e5m2"):
        byte = np.frexp(amax)[1] - 1 + 127 - (7 if fmt == "e4m3" else 14)
    else:
        mant, ex = np.frexp(amax / 6.0)
        byte = np.where(mant > 0.5, ex, ex - 1) + 127
    byte = np.clip(np.where(amax > 0, byte, 1), 1, 254)
    scaled = (w * np.exp2(127.0 - byte)[:, None, :]).reshape(k, n).astype(np.float32)
    by_word = np.ascontiguousarray(scaled.reshape(k // 512, 128, 4, n).transpose(0, 1, 3, 2))
    if fmt in ("e4m3", "e5m2"):
        words = by_word.astype(ml_dtypes.float8_e4m3fn if fmt == "e4m3" else ml_dtypes.float8_e5m2).view(np.uint8)
    else:
        c = by_word.astype(ml_dtypes.float4_e2m1fn).view(np.uint8) & 0xF
        words = c[..., 0::2] | (c[..., 1::2] << 4)
    return np.ascontiguousarray(words), np.ascontiguousarray(byte.astype(np.uint8).reshape(k // 512, 16, n))


def unpack_weight(words, scales, fmt):
    g, p, n, _ = words.shape
    if fmt in ("e4m3", "e5m2"):
        vals = np.ascontiguousarray(words).view(ml_dtypes.float8_e4m3fn if fmt == "e4m3" else ml_dtypes.float8_e5m2).astype(np.float64)
    else:
        nib = np.empty((g, p, n, 4), np.uint8)
        nib[..., 0::2] = words & 0xF
        nib[..., 1::2] = words >> 4
        vals = E2M1[nib]
    vals = vals * np.repeat(np.exp2(scales.astype(np.float64) - 127.0), 8, axis=1)[..., None]
    return vals.transpose(0, 1, 3, 2).reshape(g * 512, n)


K, H, N, T, S, T2 = 1024, 1024, 1024, 2048, 1024, 2048

def setup_inputs():
    n = np.random.standard_normal
    s = mx_kscale(K)[:, None]
    u = mx_kscale(H)[:, None]
    tab_words, tab_scales = pack_weight(n((K, T)) * np.exp(1.0 * n((1, T))) * s, "e5m2")
    w2_words, w2_scales = pack_weight(n((H, N)) / np.sqrt(H) / u, "e4m3")
    return {
        "tab_words": tab_words, "tab_scales": tab_scales,
        "offs": striped(np.random.permutation(T)[:S]),
        "offs2": striped(np.random.permutation(T2)[:S]),
        "sT": (1.0 / (1.0 + np.exp(-n((H, T))))).astype(np.float32),
        "w1": (n((K, H)) / np.sqrt(K) / s).astype(np.float32),
        "w2_words": w2_words, "w2_scales": w2_scales,
        "beta": (4.0 * np.exp(0.3 * n(H)) * u[:, 0]).astype(np.float32),
        "wgo": np.exp(0.3 * n((128, S))).astype(np.float32),
    }

def reference(tab_words, tab_scales, offs, offs2, sT, w1, w2_words, w2_scales, beta, wgo):
    v = unpack_weight(tab_words, tab_scales, "e5m2")[:, unstriped(offs)]
    h = mxq(f64(w1), 0, "e4m3").T @ v
    x = f64(sT)[:, unstriped(offs)]
    d = f64(beta)[:, None] * (x * (1.0 - x)) * h
    w2 = unpack_weight(w2_words, w2_scales, "e4m3")
    y = (w2.T @ mxq(d, 0, "e4m3")) + h
    out = np.zeros((N, T2))
    out[:, unstriped(offs2)] = np.tile(f64(wgo), (N // 128, 1)) * y
    return out

@@ -1,0 +1,287 @@
+from contextlib import ExitStack
+
+import concourse.mybir as mybir
+from concourse.masks import make_identity
+
+K, H, N, T, S, T2 = 1024, 1024, 1024, 2048, 1024, 2048
+FLOPS = 2 * K * H * S + 2 * H * N * S
+
+F32 = mybir.dt.float32
+BF16 = mybir.dt.bfloat16
+I32 = mybir.dt.int32
+U32 = mybir.dt.uint32
+U16 = mybir.dt.uint16
+U8 = mybir.dt.uint8
+E4M3 = mybir.dt.float8_e4m3fn_x4
+E5M2 = mybir.dt.float8_e5m2_x4
+MULT = mybir.AluOpType.mult
+IDENT = mybir.ActivationFunctionType.Identity
+
+P = 128
+PACK = 4
+PASS = P * PACK
+BANK = 512
+HALF = S // 2
+QUADS = 4
+AL = 64
+STAG = {(1, 2): "A", (1, 3): "B"}
+DTAG = {(1, 0): "A", (1, 1): "A", (0, 0): "B", (0, 1): "B"}
+
+
+def tile_list_leak_residual_backward_kernel(
+    tc, tab_words, tab_scales, offs, offs2, sT, w1, w2_words, w2_scales, beta, wgo, out
+):
+    nc = tc.nc
+    passes = K // PASS
+    blocks = S // P
+    with ExitStack() as ctx:
+        lists = ctx.enter_context(tc.tile_pool(name="lists", bufs=1))
+        keep = ctx.enter_context(tc.tile_pool(name="keep", bufs=1))
+        ring = ctx.enter_context(tc.tile_pool(name="ring", bufs=6))
+        rows = ctx.enter_context(tc.tile_pool(name="rows", bufs=6))
+        held = ctx.enter_context(tc.tile_pool(name="held", bufs=1))
+        stage = ctx.enter_context(tc.tile_pool(name="stage", bufs=2))
+        psum = ctx.enter_context(tc.psum_pool(name="psum", bufs=1))
+
+        idx = lists.tile([P, S // 16], U16, name="idx")
+        idx2 = lists.tile([P, S // 16], U16, name="idx2")
+        s_rows = sT.rearrange("(b p t) c -> b t p c", b=passes, t=PACK)
+        out_rows = out.rearrange("(b p t) c -> b t p c", b=passes, t=PACK)
+
+        tab_plane = keep.tile([P, passes * T], U8, name="tab_plane", align_bytes=AL)
+        nc.gpsimd.memset(tab_plane[:].bitcast(I32), 0)
+        nc.sync.dma_start(idx[:], offs)
+
+        slope = keep.tile([P, passes, PACK], F32, name="slope")
+        neg_slope = keep.tile([P, passes, PACK], F32, name="neg_slope")
+        nc.scalar.dma_start(slope[:], beta.rearrange("(b p t) -> p b t", b=passes, t=PACK))
+        nc.scalar.activation(neg_slope[:], slope[:], IDENT, scale=-1.0)
+
+        def load_planes(plane, scales):
+            for q in range(QUADS):
+                nc.sync.dma_start(
+                    plane[32 * q : 32 * q + 4 * passes, :].bitcast(I32),
+                    scales[:, 4 * q : 4 * q + 4, :].bitcast(I32),
+                )
+
+        gates = {}
+        for b in range(passes):
+            for half in range(2):
+                gates[b, half] = keep.tile([P, PACK, HALF], F32, name="gate%d%d" % (b, half), align_bytes=AL)
+
+        def gate_rows(b, t, pieces):
+            if (b, t) in STAG:
+                window = held.tile([P, T], F32, name="s_window", tag=STAG[b, t], align_bytes=AL)
+            else:
+                window = ring.tile([P, T], F32, name="s_window", tag="big", align_bytes=AL)
+            nc.sync.dma_start(window[:], s_rows[b, t])
+            x = rows.tile([P, S], F32, name="x", tag="row", align_bytes=AL)
+            width = S // pieces
+            for c in range(pieces):
+                nc.vector.tensor_copy(
+                    x[:, c * width : (c + 1) * width],
+                    window[:].indirect(idx[:, c * width // 16 : (c + 1) * width // 16]),
+                )
+            for half in range(2):
+                gate = gates[b, half][:, t, :]
+                xs = x[:, half * HALF : (half + 1) * HALF]
+                nc.scalar.activation(gate, xs, IDENT, bias=slope[:, b, t : t + 1], scale=neg_slope[:, b, t : t + 1])
+                nc.gpsimd.tensor_tensor(gate, gate, xs, MULT)
+
+        v_words = []
+
+        def table_words(a):
+            window = ring.tile([P, T], U32, name="tab_window", tag="big", align_bytes=AL)
+            nc.sync.dma_start(window[:].bitcast(I32), tab_words[a].rearrange("p t i -> p (t i)").bitcast(I32))
+            words = keep.tile([P, S], U32, name="v_words%d" % a, align_bytes=AL)
+            nc.vector.tensor_copy(words[:], window[:].indirect(idx[:]))
+            v_words.append(words)
+
+        v_plane0 = keep.tile([P, S], U8, name="v_plane0", align_bytes=AL)
+        v_plane1 = keep.tile([P, S], U8, name="v_plane1", align_bytes=AL)
+        v_planes = [v_plane0, v_plane1]
+
+        def table_planes():
+            for q in range(QUADS):
+                nc.sync.dma_start(
+                    tab_plane[32 * q : 32 * q + 4, :].bitcast(I32).rearrange("r (a w) -> r a w", a=passes),
+                    tab_scales[:, 4 * q : 4 * q + 4, :].bitcast(I32).rearrange("a r w -> r a w"),
+                )
+            for a in range(passes):
+                nc.vector.tensor_copy(v_planes[a][:], tab_plane[:, a * T : (a + 1) * T].indirect(idx[:]))
+
+        w1_words = {}
+        w1_planes = {}
+
+        def quantize_w1(a, b):
+            raw = ring.tile([P, PACK, BANK], F32, name="w1_raw", tag="big", align_bytes=AL)
+            nc.sync.dma_start(
+                raw[:],
+                w1[a * PASS : (a + 1) * PASS, b * BANK : (b + 1) * BANK].rearrange("(p t) c -> p t c", t=PACK),
+            )
+            woven = rows.tile([P, PACK * BANK], BF16, name="w1_woven", tag="row", align_bytes=AL)
+            nc.scalar.copy(
+                woven[:].rearrange("p (c i t) -> p c t i", i=4, t=PACK),
+                raw[:].rearrange("p t (c i) -> p c t i", i=4),
+            )
+            words = keep.tile([P, BANK], U32, name="w1_words%d%d" % (a, b), align_bytes=AL)
+            plane = keep.tile([P, BANK], U8, name="w1_plane%d%d" % (a, b), align_bytes=AL)
+            nc.vector.quantize_mx(words[:].bitcast(E4M3), plane[:], woven[:])
+            w1_words[a, b] = words
+            w1_planes[a, b] = plane
+
+        h_t = {}
+
+        def first_product(b):
+            for jb in range(blocks):
+                cols = slice(jb * P, (jb + 1) * P)
+                acc = psum.tile([P, BANK], F32, name="acc", tag="mx", bufs=3)
+                for a in range(passes):
+                    nc.tensor.matmul_mx(
+                        acc[:],
+                        lhsT=v_words[a][:, cols].bitcast(E5M2),
+                        lhsT_scale=v_planes[a][:, cols],
+                        rhs=w1_words[a, b][:].bitcast(E4M3),
+                        rhs_scale=w1_planes[a, b][:],
+                        start=(a == 0),
+                        stop=(a == passes - 1),
+                    )
+                ht = keep.tile([P, BANK], F32, name="h_t%d%d" % (b, jb), align_bytes=AL)
+                nc.scalar.copy(
+                    ht[:].rearrange("p (t m) -> p t m", t=PACK), acc[:].rearrange("p (m t) -> p t m", t=PACK)
+                )
+                h_t[b, jb] = ht
+
+        d_words = {}
+        d_planes = {}
+
+        def quantize_d(b, half):
+            woven = held.tile([P, PACK * HALF], BF16, name="d_woven", tag=DTAG[b, half], align_bytes=AL)
+            for q in range(blocks // 2):
+                ht = h_t[b, half * (blocks // 2) + q]
+                hb = psum.tile([P, PACK, P], F32, name="hb", tag="hb", bufs=3)
+                for t in range(PACK):
+                    nc.tensor.transpose(hb[:, t, :], ht[:, t * P : (t + 1) * P], ident[:])
+                nc.vector.tensor_tensor(
+                    woven[:, q * BANK : (q + 1) * BANK].rearrange("p (c i t) -> p c t i", i=4, t=PACK),
+                    hb[:].rearrange("p t (c i) -> p c t i", i=4),
+                    gates[b, half][:, :, q * P : (q + 1) * P].rearrange("p t (c i) -> p c t i", i=4),
+                    MULT,
+                )
+            words = keep.tile([P, HALF], U32, name="d_words%d%d" % (b, half), align_bytes=AL)
+            plane = keep.tile([P, HALF], U8, name="d_plane%d%d" % (b, half), align_bytes=AL)
+            nc.vector.quantize_mx(words[:].bitcast(E4M3), plane[:], woven[:])
+            d_words[b, half] = words
+            d_planes[b, half] = plane
+
+        ident = keep.tile([P, P], F32, name="ident")
+        w2_plane = keep.tile([P, N], U8, name="w2_plane", align_bytes=AL)
+        pages = []
+
+        def constants():
+            make_identity(nc, ident[:])
+            nc.gpsimd.memset(w2_plane[:].bitcast(I32), 0)
+            for t in range(PACK):
+                page = keep.tile([P, T2], F32, name="page%d" % t, align_bytes=AL)
+                nc.gpsimd.memset(page[:], 0.0)
+                pages.append(page)
+
+        w2_tiles = []
+        weights = []
+
+        def late_loads():
+            for a in range(passes):
+                words = keep.tile([P, N], U32, name="w2_words%d" % a, align_bytes=AL)
+                nc.sync.dma_start(words[:].bitcast(I32), w2_words[a].rearrange("p n i -> p (n i)").bitcast(I32))
+                w2_tiles.append(words)
+            load_planes(w2_plane, w2_scales)
+            nc.sync.dma_start(idx2[:], offs2)
+            wgo_rows = wgo.rearrange("(q t) j -> t q j", t=PACK)
+            for t in range(PACK):
+                weight = rows.tile([P, S], F32, name="weight", tag="row", align_bytes=AL)
+                for q in range(QUADS):
+                    nc.sync.dma_start(weight[32 * q : 32 * (q + 1), :], wgo_rows[t])
+                weights.append(weight)
+
+        m_t = {}
+
+        def second_product(b, half):
+            cols_n = slice(b * BANK, (b + 1) * BANK)
+            mt = ring.tile([P, blocks // 2, BANK], F32, name="m_t", tag="big", align_bytes=AL)
+            for q in range(blocks // 2):
+                cols = slice(q * P, (q + 1) * P)
+                acc = psum.tile([P, BANK], F32, name="acc", tag="mx", bufs=3)
+                for a in range(passes):
+                    nc.tensor.matmul_mx(
+                        acc[:],
+                        lhsT=d_words[a, half][:, cols].bitcast(E4M3),
+                        lhsT_scale=d_planes[a, half][:, cols],
+                        rhs=w2_tiles[a][:, cols_n].bitcast(E4M3),
+                        rhs_scale=w2_plane[4 * a : P, cols_n],
+                        start=(a == 0),
+                        stop=(a == passes - 1),
+                    )
+                nc.scalar.copy(
+                    mt[:, q, :].rearrange("p (t m) -> p t m", t=PACK),
+                    acc[:].rearrange("p (m t) -> p t m", t=PACK),
+                )
+            m_t[b, half] = mt
+
+        def place(b, half, t):
+            yb = psum.tile([P, HALF], F32, name="yb", tag="yb", bufs=2)
+            for q in range(blocks // 2):
+                jb = half * (blocks // 2) + q
+                nc.tensor.matmul(
+                    yb[:, q * P : (q + 1) * P], h_t[b, jb][:, t * P : (t + 1) * P], ident[:],
+                    start=True, stop=False, is_transpose=True,
+                )
+                nc.tensor.matmul(
+                    yb[:, q * P : (q + 1) * P], m_t[b, half][:, q, t * P : (t + 1) * P], ident[:],
+                    start=False, stop=True, is_transpose=True,
+                )
+            y = stage.tile([P, HALF], F32, name="y", bufs=3, align_bytes=AL)
+            nc.scalar.copy(y[:], yb[:])
+            nc.vector.tensor_tensor(
+                pages[t][:].indirect(idx2[:, half * (HALF // 16) : (half + 1) * (HALF // 16)]),
+                y[:],
+                weights[t][:, half * HALF : (half + 1) * HALF],
+                MULT,
+            )
+            if half == 1:
+                nc.sync.dma_start(out_rows[b, t], pages[t][:])
+
+        def place_all(b):
+            for pair in range(PACK // 2):
+                for half in range(2):
+                    for t in (2 * pair, 2 * pair + 1):
+                        place(b, half, t)
+
+        gate_rows(0, 0, 1)
+        table_planes()
+        constants()
+        table_words(0)
+        table_words(1)
+        quantize_w1(0, 0)
+        quantize_w1(1, 0)
+        quantize_w1(0, 1)
+        quantize_w1(1, 1)
+        gate_rows(0, 1, 1)
+        gate_rows(0, 2, 1)
+        gate_rows(0, 3, 1)
+        gate_rows(1, 0, 1)
+        gate_rows(1, 1, 1)
+        gate_rows(1, 2, 1)
+        gate_rows(1, 3, 2)
+        first_product(0)
+        first_product(1)
+        late_loads()
+        quantize_d(0, 0)
+        quantize_d(1, 0)
+        second_product(0, 0)
+        quantize_d(0, 1)
+        quantize_d(1, 1)
+        second_product(0, 1)
+        place_all(0)
+        second_product(1, 0)
+        second_product(1, 1)
+        place_all(1)

@@ -24,8 +24,8 @@ BANK = 512
 HALF = S // 2
 QUADS = 4
 AL = 64
-STAG = {(1, 2): "A", (1, 3): "B"}
-DTAG = {(1, 0): "A", (1, 1): "A", (0, 0): "B", (0, 1): "B"}
+RUN = 2
+STAG = {(1, 2): "A", (1, 3): "B", (0, 1): "C"}
 
 
 def tile_list_leak_residual_backward_kernel(
@@ -38,7 +38,7 @@ def tile_list_leak_residual_backward_kernel(
         lists = ctx.enter_context(tc.tile_pool(name="lists", bufs=1))
         keep = ctx.enter_context(tc.tile_pool(name="keep", bufs=1))
         ring = ctx.enter_context(tc.tile_pool(name="ring", bufs=6))
-        rows = ctx.enter_context(tc.tile_pool(name="rows", bufs=6))
+        rows = ctx.enter_context(tc.tile_pool(name="rows", bufs=5))
         held = ctx.enter_context(tc.tile_pool(name="held", bufs=1))
         stage = ctx.enter_context(tc.tile_pool(name="stage", bufs=2))
         psum = ctx.enter_context(tc.psum_pool(name="psum", bufs=1))
@@ -64,10 +64,7 @@ def tile_list_leak_residual_backward_kernel(
                     scales[:, 4 * q : 4 * q + 4, :].bitcast(I32),
                 )
 
-        gates = {}
-        for b in range(passes):
-            for half in range(2):
-                gates[b, half] = keep.tile([P, PACK, HALF], F32, name="gate%d%d" % (b, half), align_bytes=AL)
+        gates = [keep.tile([P, 2, PACK, HALF], F32, name="gate%d" % b, align_bytes=AL) for b in range(passes)]
 
         def gate_rows(b, t, pieces):
             if (b, t) in STAG:
@@ -75,18 +72,19 @@ def tile_list_leak_residual_backward_kernel(
             else:
                 window = ring.tile([P, T], F32, name="s_window", tag="big", align_bytes=AL)
             nc.sync.dma_start(window[:], s_rows[b, t])
-            x = rows.tile([P, S], F32, name="x", tag="row", align_bytes=AL)
-            width = S // pieces
+            x = rows.tile([P, 2, HALF], F32, name="x", tag="row", align_bytes=AL)
+            halves = 2 // pieces
             for c in range(pieces):
-                nc.vector.tensor_copy(
-                    x[:, c * width : (c + 1) * width],
-                    window[:].indirect(idx[:, c * width // 16 : (c + 1) * width // 16]),
+                part = slice(c * halves, (c + 1) * halves)
+                entries = slice(c * halves * HALF // 16, (c + 1) * halves * HALF // 16)
+                nc.vector.tensor_copy(x[:, part, :].rearrange("p h j -> p (h j)"), window[:].indirect(idx[:, entries]))
+            for c in range(pieces):
+                part = slice(c * halves, (c + 1) * halves)
+                gate = gates[b][:, part, t, :]
+                nc.scalar.activation(
+                    gate, x[:, part, :], IDENT, bias=slope[:, b, t : t + 1], scale=neg_slope[:, b, t : t + 1]
                 )
-            for half in range(2):
-                gate = gates[b, half][:, t, :]
-                xs = x[:, half * HALF : (half + 1) * HALF]
-                nc.scalar.activation(gate, xs, IDENT, bias=slope[:, b, t : t + 1], scale=neg_slope[:, b, t : t + 1])
-                nc.gpsimd.tensor_tensor(gate, gate, xs, MULT)
+                nc.gpsimd.tensor_tensor(gate, gate, x[:, part, :], MULT)
 
         v_words = []
 
@@ -113,7 +111,9 @@ def tile_list_leak_residual_backward_kernel(
         w1_words = {}
         w1_planes = {}
 
-        def quantize_w1(a, b):
+        w1_woven = {}
+
+        def weave_w1(a, b):
             raw = ring.tile([P, PACK, BANK], F32, name="w1_raw", tag="big", align_bytes=AL)
             nc.sync.dma_start(
                 raw[:],
@@ -121,12 +121,18 @@ def tile_list_leak_residual_backward_kernel(
             )
             woven = rows.tile([P, PACK * BANK], BF16, name="w1_woven", tag="row", align_bytes=AL)
             nc.scalar.copy(
-                woven[:].rearrange("p (c i t) -> p c t i", i=4, t=PACK),
-                raw[:].rearrange("p t (c i) -> p c t i", i=4),
+                woven[:].rearrange("p (c i t) -> p c t i", i=RUN, t=PACK),
+                raw[:].rearrange("p t (c i) -> p c t i", i=RUN),
             )
-            words = keep.tile([P, BANK], U32, name="w1_words%d%d" % (a, b), align_bytes=AL)
+            w1_woven[a, b] = woven
+
+        def quantize_w1(a, b):
+            if (a, b) == (1, 1):
+                words = held.tile([P, BANK], U32, name="w1_words11", tag="C", align_bytes=AL)
+            else:
+                words = keep.tile([P, BANK], U32, name="w1_words%d%d" % (a, b), align_bytes=AL)
             plane = keep.tile([P, BANK], U8, name="w1_plane%d%d" % (a, b), align_bytes=AL)
-            nc.vector.quantize_mx(words[:].bitcast(E4M3), plane[:], woven[:])
+            nc.vector.quantize_mx(words[:].bitcast(E4M3), plane[:], w1_woven[a, b][:])
             w1_words[a, b] = words
             w1_planes[a, b] = plane
 
@@ -135,7 +141,7 @@ def tile_list_leak_residual_backward_kernel(
         def first_product(b):
             for jb in range(blocks):
                 cols = slice(jb * P, (jb + 1) * P)
-                acc = psum.tile([P, BANK], F32, name="acc", tag="mx", bufs=3)
+                acc = psum.tile([P, BANK], F32, name="acc", tag="mx", bufs=2)
                 for a in range(passes):
                     nc.tensor.matmul_mx(
                         acc[:],
@@ -155,24 +161,26 @@ def tile_list_leak_residual_backward_kernel(
         d_words = {}
         d_planes = {}
 
-        def quantize_d(b, half):
-            woven = held.tile([P, PACK * HALF], BF16, name="d_woven", tag=DTAG[b, half], align_bytes=AL)
-            for q in range(blocks // 2):
-                ht = h_t[b, half * (blocks // 2) + q]
-                hb = psum.tile([P, PACK, P], F32, name="hb", tag="hb", bufs=3)
+        def quantize_d(b, first, count, tag):
+            woven = held.tile([P, count * BANK], BF16, name="d_woven", tag=tag, align_bytes=AL)
+            for q in range(count):
+                jb = first + q
+                half, col = divmod(jb * P, HALF)
+                hb = psum.tile([P, PACK, P], F32, name="hb", tag="hb", bufs=4)
                 for t in range(PACK):
-                    nc.tensor.transpose(hb[:, t, :], ht[:, t * P : (t + 1) * P], ident[:])
+                    nc.tensor.transpose(hb[:, t, :], h_t[b, jb][:, t * P : (t + 1) * P], ident[:])
                 nc.vector.tensor_tensor(
-                    woven[:, q * BANK : (q + 1) * BANK].rearrange("p (c i t) -> p c t i", i=4, t=PACK),
-                    hb[:].rearrange("p t (c i) -> p c t i", i=4),
-                    gates[b, half][:, :, q * P : (q + 1) * P].rearrange("p t (c i) -> p c t i", i=4),
+                    woven[:, q * BANK : (q + 1) * BANK].rearrange("p (c i t) -> p c t i", i=RUN, t=PACK),
+                    hb[:].rearrange("p t (c i) -> p c t i", i=RUN),
+                    gates[b][:, half, :, col : col + P].rearrange("p t (c i) -> p c t i", i=RUN),
                     MULT,
                 )
-            words = keep.tile([P, HALF], U32, name="d_words%d%d" % (b, half), align_bytes=AL)
-            plane = keep.tile([P, HALF], U8, name="d_plane%d%d" % (b, half), align_bytes=AL)
+            words = keep.tile([P, count * P], U32, name="d_words%d%d" % (b, first), align_bytes=AL)
+            plane = keep.tile([P, count * P], U8, name="d_plane%d%d" % (b, first), align_bytes=AL)
             nc.vector.quantize_mx(words[:].bitcast(E4M3), plane[:], woven[:])
-            d_words[b, half] = words
-            d_planes[b, half] = plane
+            for q in range(count):
+                d_words[b, first + q] = words[:, q * P : (q + 1) * P]
+                d_planes[b, first + q] = plane[:, q * P : (q + 1) * P]
 
         ident = keep.tile([P, P], F32, name="ident")
         w2_plane = keep.tile([P, N], U8, name="w2_plane", align_bytes=AL)
@@ -209,13 +217,13 @@ def tile_list_leak_residual_backward_kernel(
             cols_n = slice(b * BANK, (b + 1) * BANK)
             mt = ring.tile([P, blocks // 2, BANK], F32, name="m_t", tag="big", align_bytes=AL)
             for q in range(blocks // 2):
-                cols = slice(q * P, (q + 1) * P)
-                acc = psum.tile([P, BANK], F32, name="acc", tag="mx", bufs=3)
+                jb = half * (blocks // 2) + q
+                acc = psum.tile([P, BANK], F32, name="acc", tag="mx", bufs=2)
                 for a in range(passes):
                     nc.tensor.matmul_mx(
                         acc[:],
-                        lhsT=d_words[a, half][:, cols].bitcast(E4M3),
-                        lhsT_scale=d_planes[a, half][:, cols],
+                        lhsT=d_words[a, jb].bitcast(E4M3),
+                        lhsT_scale=d_planes[a, jb],
                         rhs=w2_tiles[a][:, cols_n].bitcast(E4M3),
                         rhs_scale=w2_plane[4 * a : P, cols_n],
                         start=(a == 0),
@@ -227,45 +235,50 @@ def tile_list_leak_residual_backward_kernel(
                 )
             m_t[b, half] = mt
 
-        def place(b, half, t):
-            yb = psum.tile([P, HALF], F32, name="yb", tag="yb", bufs=2)
-            for q in range(blocks // 2):
-                jb = half * (blocks // 2) + q
+        def place(b, t, first, count):
+            half, q0 = divmod(first, blocks // 2)
+            yb = psum.tile([P, count * P], F32, name="yb", tag="yb", bufs=2)
+            for q in range(count):
                 nc.tensor.matmul(
-                    yb[:, q * P : (q + 1) * P], h_t[b, jb][:, t * P : (t + 1) * P], ident[:],
+                    yb[:, q * P : (q + 1) * P], h_t[b, first + q][:, t * P : (t + 1) * P], ident[:],
                     start=True, stop=False, is_transpose=True,
                 )
                 nc.tensor.matmul(
-                    yb[:, q * P : (q + 1) * P], m_t[b, half][:, q, t * P : (t + 1) * P], ident[:],
+                    yb[:, q * P : (q + 1) * P], m_t[b, half][:, q0 + q, t * P : (t + 1) * P], ident[:],
                     start=False, stop=True, is_transpose=True,
                 )
-            y = stage.tile([P, HALF], F32, name="y", bufs=3, align_bytes=AL)
+            y = stage.tile([P, count * P], F32, name="y", tag="y", bufs=3, align_bytes=AL)
             nc.scalar.copy(y[:], yb[:])
             nc.vector.tensor_tensor(
-                pages[t][:].indirect(idx2[:, half * (HALF // 16) : (half + 1) * (HALF // 16)]),
+                pages[t][:].indirect(idx2[:, first * P // 16 : (first + count) * P // 16]),
                 y[:],
-                weights[t][:, half * HALF : (half + 1) * HALF],
+                weights[t][:, first * P : (first + count) * P],
                 MULT,
             )
-            if half == 1:
+            if first + count == blocks:
                 nc.sync.dma_start(out_rows[b, t], pages[t][:])
 
         def place_all(b):
             for pair in range(PACK // 2):
-                for half in range(2):
+                runs = [(0, 2), (2, 2), (4, 4)] if (b, pair) == (0, 0) else [(0, 4), (4, 4)]
+                for first, count in runs:
                     for t in (2 * pair, 2 * pair + 1):
-                        place(b, half, t)
+                        place(b, t, first, count)
 
         gate_rows(0, 0, 1)
         table_planes()
         constants()
         table_words(0)
         table_words(1)
+        weave_w1(0, 0)
         quantize_w1(0, 0)
+        weave_w1(1, 0)
         quantize_w1(1, 0)
+        weave_w1(0, 1)
         quantize_w1(0, 1)
-        quantize_w1(1, 1)
+        weave_w1(1, 1)
         gate_rows(0, 1, 1)
+        quantize_w1(1, 1)
         gate_rows(0, 2, 1)
         gate_rows(0, 3, 1)
         gate_rows(1, 0, 1)
@@ -275,11 +288,10 @@ def tile_list_leak_residual_backward_kernel(
         first_product(0)
         first_product(1)
         late_loads()
-        quantize_d(0, 0)
-        quantize_d(1, 0)
+        quantize_d(0, 0, 8, "B")
+        quantize_d(1, 0, 4, "A")
         second_product(0, 0)
-        quantize_d(0, 1)
-        quantize_d(1, 1)
+        quantize_d(1, 4, 4, "A")
         second_product(0, 1)
         place_all(0)
         second_product(1, 0)

@@ -15,285 +15,262 @@ U8 = mybir.dt.uint8
 E4M3 = mybir.dt.float8_e4m3fn_x4
 E5M2 = mybir.dt.float8_e5m2_x4
 MULT = mybir.AluOpType.mult
-IDENT = mybir.ActivationFunctionType.Identity
+IDENTITY = mybir.ActivationFunctionType.Identity
 
 P = 128
 PACK = 4
 PASS = P * PACK
+PASSES = K // PASS
 BANK = 512
+QUAD = 32
+QUADS = P // QUAD
+PLANE_ROWS = 4
+BLOCKS = S // P
 HALF = S // 2
-QUADS = 4
-AL = 64
+HALF_BLOCKS = BLOCKS // 2
+PER_COLUMN = 16
+ALIGN = 64
 RUN = 2
-STAG = {(1, 2): "A", (1, 3): "B", (0, 1): "C"}
+PAGES = 3
+
+WINDOW_BUFS = 6
+ROW_BUFS = 5
+Y_BUFS = 3
+MX_BANKS, H_BANKS, Y_BANKS = 3, 3, 2
 
 
 def tile_list_leak_residual_backward_kernel(
     tc, tab_words, tab_scales, offs, offs2, sT, w1, w2_words, w2_scales, beta, wgo, out
 ):
     nc = tc.nc
-    passes = K // PASS
-    blocks = S // P
     with ExitStack() as ctx:
         lists = ctx.enter_context(tc.tile_pool(name="lists", bufs=1))
         keep = ctx.enter_context(tc.tile_pool(name="keep", bufs=1))
-        ring = ctx.enter_context(tc.tile_pool(name="ring", bufs=6))
-        rows = ctx.enter_context(tc.tile_pool(name="rows", bufs=5))
-        held = ctx.enter_context(tc.tile_pool(name="held", bufs=1))
-        stage = ctx.enter_context(tc.tile_pool(name="stage", bufs=2))
+        windows = ctx.enter_context(tc.tile_pool(name="windows", bufs=WINDOW_BUFS))
+        rows = ctx.enter_context(tc.tile_pool(name="rows", bufs=ROW_BUFS))
+        turns = ctx.enter_context(tc.tile_pool(name="turns", bufs=1))
+        staged = ctx.enter_context(tc.tile_pool(name="staged", bufs=Y_BUFS))
         psum = ctx.enter_context(tc.psum_pool(name="psum", bufs=1))
 
-        idx = lists.tile([P, S // 16], U16, name="idx")
-        idx2 = lists.tile([P, S // 16], U16, name="idx2")
-        s_rows = sT.rearrange("(b p t) c -> b t p c", b=passes, t=PACK)
-        out_rows = out.rearrange("(b p t) c -> b t p c", b=passes, t=PACK)
+        idx = lists.tile([P, S // PER_COLUMN], U16, name="idx")
+        idx2 = lists.tile([P, S // PER_COLUMN], U16, name="idx2")
+        s_rows = sT.rearrange("(b p t) c -> b t p c", b=PASSES, t=PACK)
+        out_rows = out.rearrange("(b p t) c -> b t p c", b=PASSES, t=PACK)
 
-        tab_plane = keep.tile([P, passes * T], U8, name="tab_plane", align_bytes=AL)
-        nc.gpsimd.memset(tab_plane[:].bitcast(I32), 0)
+        tab_planes = keep.tile([P, PASSES * T], U8, name="tab_planes", align_bytes=ALIGN)
+        nc.gpsimd.memset(tab_planes[:].bitcast(I32), 0)
         nc.sync.dma_start(idx[:], offs)
 
-        slope = keep.tile([P, passes, PACK], F32, name="slope")
-        neg_slope = keep.tile([P, passes, PACK], F32, name="neg_slope")
-        nc.scalar.dma_start(slope[:], beta.rearrange("(b p t) -> p b t", b=passes, t=PACK))
-        nc.scalar.activation(neg_slope[:], slope[:], IDENT, scale=-1.0)
+        slope = keep.tile([P, PASSES, PACK], F32, name="slope")
+        neg_slope = keep.tile([P, PASSES, PACK], F32, name="neg_slope")
+        nc.scalar.dma_start(slope[:], beta.rearrange("(b p t) -> p b t", b=PASSES, t=PACK))
+        nc.scalar.activation(neg_slope[:], slope[:], IDENTITY, scale=-1.0)
 
-        def load_planes(plane, scales):
-            for q in range(QUADS):
-                nc.sync.dma_start(
-                    plane[32 * q : 32 * q + 4 * passes, :].bitcast(I32),
-                    scales[:, 4 * q : 4 * q + 4, :].bitcast(I32),
-                )
+        gates = [keep.tile([P, 2, PACK, HALF], F32, name="gate%d" % b, align_bytes=ALIGN) for b in range(PASSES)]
 
-        gates = [keep.tile([P, 2, PACK, HALF], F32, name="gate%d" % b, align_bytes=AL) for b in range(passes)]
-
-        def gate_rows(b, t, pieces):
-            if (b, t) in STAG:
-                window = held.tile([P, T], F32, name="s_window", tag=STAG[b, t], align_bytes=AL)
-            else:
-                window = ring.tile([P, T], F32, name="s_window", tag="big", align_bytes=AL)
+        def make_gate(b, t, window, pieces=1):
             nc.sync.dma_start(window[:], s_rows[b, t])
-            x = rows.tile([P, 2, HALF], F32, name="x", tag="row", align_bytes=AL)
+            x = rows.tile([P, 2, HALF], F32, name="x", tag="row", align_bytes=ALIGN)
             halves = 2 // pieces
+            columns = S // PER_COLUMN // pieces
             for c in range(pieces):
-                part = slice(c * halves, (c + 1) * halves)
-                entries = slice(c * halves * HALF // 16, (c + 1) * halves * HALF // 16)
-                nc.vector.tensor_copy(x[:, part, :].rearrange("p h j -> p (h j)"), window[:].indirect(idx[:, entries]))
-            for c in range(pieces):
-                part = slice(c * halves, (c + 1) * halves)
-                gate = gates[b][:, part, t, :]
-                nc.scalar.activation(
-                    gate, x[:, part, :], IDENT, bias=slope[:, b, t : t + 1], scale=neg_slope[:, b, t : t + 1]
+                nc.vector.tensor_copy(
+                    x[:, c * halves : (c + 1) * halves, :].rearrange("p h j -> p (h j)"),
+                    window[:].indirect(idx[:, c * columns : (c + 1) * columns]),
                 )
-                nc.gpsimd.tensor_tensor(gate, gate, x[:, part, :], MULT)
+            for c in range(pieces):
+                xs = x[:, c * halves : (c + 1) * halves, :]
+                gate = gates[b][:, c * halves : (c + 1) * halves, t, :]
+                nc.scalar.activation(gate, xs, IDENTITY, bias=slope[:, b, t : t + 1], scale=neg_slope[:, b, t : t + 1])
+                nc.gpsimd.tensor_tensor(gate, gate, xs, MULT)
+
+        def streamed_window():
+            return windows.tile([P, T], F32, name="s_window", tag="window", align_bytes=ALIGN)
+
+        def turn_window(turn):
+            return turns.tile([P, T], F32, name="s_window", tag=turn, align_bytes=ALIGN)
+
+        make_gate(0, 0, streamed_window())
+
+        v_planes = [keep.tile([P, S], U8, name="v_plane%d" % a, align_bytes=ALIGN) for a in range(PASSES)]
+        for q in range(QUADS):
+            nc.sync.dma_start(
+                tab_planes[QUAD * q : QUAD * q + PLANE_ROWS, :].bitcast(I32).rearrange("r (a w) -> r a w", a=PASSES),
+                tab_scales[:, PLANE_ROWS * q : PLANE_ROWS * (q + 1), :].bitcast(I32).rearrange("a r w -> r a w"),
+            )
+        for a in range(PASSES):
+            nc.vector.tensor_copy(v_planes[a][:], tab_planes[:, a * T : (a + 1) * T].indirect(idx[:]))
+
+        identity = keep.tile([P, P], F32, name="identity")
+        make_identity(nc, identity[:])
+        w2_planes = keep.tile([P, N], U8, name="w2_planes", align_bytes=ALIGN)
+        nc.gpsimd.memset(w2_planes[:].bitcast(I32), 0)
+        pages = [keep.tile([P, T2], F32, name="page%d" % i, align_bytes=ALIGN) for i in range(PAGES)]
+        for page in pages:
+            nc.gpsimd.memset(page[:], 0.0)
 
         v_words = []
-
-        def table_words(a):
-            window = ring.tile([P, T], U32, name="tab_window", tag="big", align_bytes=AL)
-            nc.sync.dma_start(window[:].bitcast(I32), tab_words[a].rearrange("p t i -> p (t i)").bitcast(I32))
-            words = keep.tile([P, S], U32, name="v_words%d" % a, align_bytes=AL)
+        for a in range(PASSES):
+            window = windows.tile([P, T], U32, name="tab_window", tag="window", align_bytes=ALIGN)
+            nc.sync.dma_start(window[:].bitcast(I32), tab_words[a].rearrange("p c i -> p (c i)").bitcast(I32))
+            words = keep.tile([P, S], U32, name="v_words%d" % a, align_bytes=ALIGN)
             nc.vector.tensor_copy(words[:], window[:].indirect(idx[:]))
             v_words.append(words)
 
-        v_plane0 = keep.tile([P, S], U8, name="v_plane0", align_bytes=AL)
-        v_plane1 = keep.tile([P, S], U8, name="v_plane1", align_bytes=AL)
-        v_planes = [v_plane0, v_plane1]
-
-        def table_planes():
-            for q in range(QUADS):
-                nc.sync.dma_start(
-                    tab_plane[32 * q : 32 * q + 4, :].bitcast(I32).rearrange("r (a w) -> r a w", a=passes),
-                    tab_scales[:, 4 * q : 4 * q + 4, :].bitcast(I32).rearrange("a r w -> r a w"),
-                )
-            for a in range(passes):
-                nc.vector.tensor_copy(v_planes[a][:], tab_plane[:, a * T : (a + 1) * T].indirect(idx[:]))
-
-        w1_words = {}
-        w1_planes = {}
-
-        w1_woven = {}
-
         def weave_w1(a, b):
-            raw = ring.tile([P, PACK, BANK], F32, name="w1_raw", tag="big", align_bytes=AL)
+            raw = windows.tile([P, PACK, BANK], F32, name="w1_raw", tag="window", align_bytes=ALIGN)
             nc.sync.dma_start(
                 raw[:],
                 w1[a * PASS : (a + 1) * PASS, b * BANK : (b + 1) * BANK].rearrange("(p t) c -> p t c", t=PACK),
             )
-            woven = rows.tile([P, PACK * BANK], BF16, name="w1_woven", tag="row", align_bytes=AL)
+            woven = rows.tile([P, PACK * BANK], BF16, name="w1_woven", tag="row", align_bytes=ALIGN)
             nc.scalar.copy(
                 woven[:].rearrange("p (c i t) -> p c t i", i=RUN, t=PACK),
                 raw[:].rearrange("p t (c i) -> p c t i", i=RUN),
             )
-            w1_woven[a, b] = woven
+            return woven
 
-        def quantize_w1(a, b):
-            if (a, b) == (1, 1):
-                words = held.tile([P, BANK], U32, name="w1_words11", tag="C", align_bytes=AL)
-            else:
-                words = keep.tile([P, BANK], U32, name="w1_words%d%d" % (a, b), align_bytes=AL)
-            plane = keep.tile([P, BANK], U8, name="w1_plane%d%d" % (a, b), align_bytes=AL)
-            nc.vector.quantize_mx(words[:].bitcast(E4M3), plane[:], w1_woven[a, b][:])
-            w1_words[a, b] = words
-            w1_planes[a, b] = plane
+        w1_mx = {}
+
+        def quantize_w1(a, b, woven, words):
+            plane = keep.tile([P, BANK], U8, name="w1_plane%d%d" % (a, b), align_bytes=ALIGN)
+            nc.vector.quantize_mx(words[:].bitcast(E4M3), plane[:], woven[:])
+            w1_mx[a, b] = (words, plane)
+
+        w1_pieces = [(a, b) for b in range(PASSES) for a in range(PASSES)]
+        for a, b in w1_pieces[:-1]:
+            woven = weave_w1(a, b)
+            quantize_w1(a, b, woven, keep.tile([P, BANK], U32, name="w1_words%d%d" % (a, b), align_bytes=ALIGN))
+        last_a, last_b = w1_pieces[-1]
+        woven = weave_w1(last_a, last_b)
+        make_gate(0, 1, turn_window("then_w1"))
+        quantize_w1(last_a, last_b, woven, turns.tile([P, BANK], U32, name="w1_last", tag="then_w1", align_bytes=ALIGN))
+
+        row_tiles = [(b, t) for b in range(PASSES) for t in range(PACK)]
+        for b, t in row_tiles[2:-2]:
+            make_gate(b, t, streamed_window())
+        make_gate(*row_tiles[-2], turn_window("then_d1"))
+        make_gate(*row_tiles[-1], turn_window("then_d0"), pieces=2)
+
+        def product(lhs, rhs, dtype):
+            acc = psum.tile([P, BANK], F32, name="acc", tag="mx", bufs=MX_BANKS)
+            for a in range(PASSES):
+                nc.tensor.matmul_mx(
+                    acc[:],
+                    lhsT=lhs[a][0].bitcast(dtype),
+                    lhsT_scale=lhs[a][1],
+                    rhs=rhs[a][0].bitcast(E4M3),
+                    rhs_scale=rhs[a][1],
+                    start=(a == 0),
+                    stop=(a == PASSES - 1),
+                )
+            return acc
+
+        def copy_by_row_tile(dst, acc):
+            nc.scalar.copy(dst.rearrange("p (t m) -> p t m", t=PACK), acc[:].rearrange("p (m t) -> p t m", t=PACK))
 
         h_t = {}
-
-        def first_product(b):
-            for jb in range(blocks):
-                cols = slice(jb * P, (jb + 1) * P)
-                acc = psum.tile([P, BANK], F32, name="acc", tag="mx", bufs=2)
-                for a in range(passes):
-                    nc.tensor.matmul_mx(
-                        acc[:],
-                        lhsT=v_words[a][:, cols].bitcast(E5M2),
-                        lhsT_scale=v_planes[a][:, cols],
-                        rhs=w1_words[a, b][:].bitcast(E4M3),
-                        rhs_scale=w1_planes[a, b][:],
-                        start=(a == 0),
-                        stop=(a == passes - 1),
-                    )
-                ht = keep.tile([P, BANK], F32, name="h_t%d%d" % (b, jb), align_bytes=AL)
-                nc.scalar.copy(
-                    ht[:].rearrange("p (t m) -> p t m", t=PACK), acc[:].rearrange("p (m t) -> p t m", t=PACK)
+        for b in range(PASSES):
+            for jb in range(BLOCKS):
+                entries = slice(jb * P, (jb + 1) * P)
+                acc = product(
+                    [(v_words[a][:, entries], v_planes[a][:, entries]) for a in range(PASSES)],
+                    [(w1_mx[a, b][0][:], w1_mx[a, b][1][:]) for a in range(PASSES)],
+                    E5M2,
                 )
-                h_t[b, jb] = ht
+                h_t[b, jb] = keep.tile([P, BANK], F32, name="h_t%d%d" % (b, jb), align_bytes=ALIGN)
+                copy_by_row_tile(h_t[b, jb][:], acc)
 
-        d_words = {}
-        d_planes = {}
+        w2_mx = []
+        for a in range(PASSES):
+            words = keep.tile([P, N], U32, name="w2_words%d" % a, align_bytes=ALIGN)
+            nc.sync.dma_start(words[:].bitcast(I32), w2_words[a].rearrange("p c i -> p (c i)").bitcast(I32))
+            w2_mx.append((words, w2_planes[PLANE_ROWS * a : P, :]))
+        for q in range(QUADS):
+            nc.sync.dma_start(
+                w2_planes[QUAD * q : QUAD * q + PLANE_ROWS * PASSES, :].bitcast(I32),
+                w2_scales[:, PLANE_ROWS * q : PLANE_ROWS * (q + 1), :].bitcast(I32),
+            )
+        nc.sync.dma_start(idx2[:], offs2)
+        wgo_rows = wgo.rearrange("(m t) j -> t m j", t=PACK)
+        weights = []
+        for t in range(PACK):
+            weight = rows.tile([P, S], F32, name="weight", tag="row", align_bytes=ALIGN)
+            for q in range(QUADS):
+                nc.sync.dma_start(weight[QUAD * q : QUAD * (q + 1), :], wgo_rows[t])
+            weights.append(weight)
 
-        def quantize_d(b, first, count, tag):
-            woven = held.tile([P, count * BANK], BF16, name="d_woven", tag=tag, align_bytes=AL)
+        d_mx = {}
+
+        def quantize_d(b, first, count, turn):
+            woven = turns.tile([P, count * BANK], BF16, name="d_woven", tag=turn, align_bytes=ALIGN)
             for q in range(count):
-                jb = first + q
-                half, col = divmod(jb * P, HALF)
-                hb = psum.tile([P, PACK, P], F32, name="hb", tag="hb", bufs=4)
+                half, column = divmod((first + q) * P, HALF)
+                h_rows = psum.tile([P, PACK, P], F32, name="h_rows", tag="h", bufs=H_BANKS)
                 for t in range(PACK):
-                    nc.tensor.transpose(hb[:, t, :], h_t[b, jb][:, t * P : (t + 1) * P], ident[:])
+                    nc.tensor.transpose(h_rows[:, t, :], h_t[b, first + q][:, t * P : (t + 1) * P], identity[:])
                 nc.vector.tensor_tensor(
                     woven[:, q * BANK : (q + 1) * BANK].rearrange("p (c i t) -> p c t i", i=RUN, t=PACK),
-                    hb[:].rearrange("p t (c i) -> p c t i", i=RUN),
-                    gates[b][:, half, :, col : col + P].rearrange("p t (c i) -> p c t i", i=RUN),
+                    h_rows[:].rearrange("p t (c i) -> p c t i", i=RUN),
+                    gates[b][:, half, :, column : column + P].rearrange("p t (c i) -> p c t i", i=RUN),
                     MULT,
                 )
-            words = keep.tile([P, count * P], U32, name="d_words%d%d" % (b, first), align_bytes=AL)
-            plane = keep.tile([P, count * P], U8, name="d_plane%d%d" % (b, first), align_bytes=AL)
+            words = keep.tile([P, count * P], U32, name="d_words%d%d" % (b, first), align_bytes=ALIGN)
+            plane = keep.tile([P, count * P], U8, name="d_plane%d%d" % (b, first), align_bytes=ALIGN)
             nc.vector.quantize_mx(words[:].bitcast(E4M3), plane[:], woven[:])
             for q in range(count):
-                d_words[b, first + q] = words[:, q * P : (q + 1) * P]
-                d_planes[b, first + q] = plane[:, q * P : (q + 1) * P]
-
-        ident = keep.tile([P, P], F32, name="ident")
-        w2_plane = keep.tile([P, N], U8, name="w2_plane", align_bytes=AL)
-        pages = []
-
-        def constants():
-            make_identity(nc, ident[:])
-            nc.gpsimd.memset(w2_plane[:].bitcast(I32), 0)
-            for t in range(PACK):
-                page = keep.tile([P, T2], F32, name="page%d" % t, align_bytes=AL)
-                nc.gpsimd.memset(page[:], 0.0)
-                pages.append(page)
-
-        w2_tiles = []
-        weights = []
-
-        def late_loads():
-            for a in range(passes):
-                words = keep.tile([P, N], U32, name="w2_words%d" % a, align_bytes=AL)
-                nc.sync.dma_start(words[:].bitcast(I32), w2_words[a].rearrange("p n i -> p (n i)").bitcast(I32))
-                w2_tiles.append(words)
-            load_planes(w2_plane, w2_scales)
-            nc.sync.dma_start(idx2[:], offs2)
-            wgo_rows = wgo.rearrange("(q t) j -> t q j", t=PACK)
-            for t in range(PACK):
-                weight = rows.tile([P, S], F32, name="weight", tag="row", align_bytes=AL)
-                for q in range(QUADS):
-                    nc.sync.dma_start(weight[32 * q : 32 * (q + 1), :], wgo_rows[t])
-                weights.append(weight)
+                d_mx[b, first + q] = (words[:, q * P : (q + 1) * P], plane[:, q * P : (q + 1) * P])
 
         m_t = {}
 
         def second_product(b, half):
-            cols_n = slice(b * BANK, (b + 1) * BANK)
-            mt = ring.tile([P, blocks // 2, BANK], F32, name="m_t", tag="big", align_bytes=AL)
-            for q in range(blocks // 2):
-                jb = half * (blocks // 2) + q
-                acc = psum.tile([P, BANK], F32, name="acc", tag="mx", bufs=2)
-                for a in range(passes):
-                    nc.tensor.matmul_mx(
-                        acc[:],
-                        lhsT=d_words[a, jb].bitcast(E4M3),
-                        lhsT_scale=d_planes[a, jb],
-                        rhs=w2_tiles[a][:, cols_n].bitcast(E4M3),
-                        rhs_scale=w2_plane[4 * a : P, cols_n],
-                        start=(a == 0),
-                        stop=(a == passes - 1),
-                    )
-                nc.scalar.copy(
-                    mt[:, q, :].rearrange("p (t m) -> p t m", t=PACK),
-                    acc[:].rearrange("p (m t) -> p t m", t=PACK),
+            columns = slice(b * BANK, (b + 1) * BANK)
+            copies = windows.tile([P, HALF_BLOCKS, BANK], F32, name="m_t", tag="window", align_bytes=ALIGN)
+            for q in range(HALF_BLOCKS):
+                jb = half * HALF_BLOCKS + q
+                acc = product(
+                    [d_mx[a, jb] for a in range(PASSES)],
+                    [(w2_mx[a][0][:, columns], w2_mx[a][1][:, columns]) for a in range(PASSES)],
+                    E4M3,
                 )
-            m_t[b, half] = mt
+                m_t[b, jb] = copies[:, q, :]
+                copy_by_row_tile(m_t[b, jb], acc)
 
         def place(b, t, first, count):
-            half, q0 = divmod(first, blocks // 2)
-            yb = psum.tile([P, count * P], F32, name="yb", tag="yb", bufs=2)
-            for q in range(count):
-                nc.tensor.matmul(
-                    yb[:, q * P : (q + 1) * P], h_t[b, first + q][:, t * P : (t + 1) * P], ident[:],
-                    start=True, stop=False, is_transpose=True,
-                )
-                nc.tensor.matmul(
-                    yb[:, q * P : (q + 1) * P], m_t[b, half][:, q0 + q, t * P : (t + 1) * P], ident[:],
-                    start=False, stop=True, is_transpose=True,
-                )
-            y = stage.tile([P, count * P], F32, name="y", tag="y", bufs=3, align_bytes=AL)
-            nc.scalar.copy(y[:], yb[:])
+            page = pages[(PACK * b + t) % PAGES]
+            columns = slice(t * P, (t + 1) * P)
+            y = staged.tile([P, count * P], F32, name="y", tag="y", align_bytes=ALIGN)
+            per_bank = min(count, BANK // P)
+            for q0 in range(0, count, per_bank):
+                sums = psum.tile([P, per_bank * P], F32, name="sums", tag="y", bufs=Y_BANKS)
+                for q in range(per_bank):
+                    jb = first + q0 + q
+                    block = sums[:, q * P : (q + 1) * P]
+                    nc.tensor.matmul(block, h_t[b, jb][:, columns], identity[:], start=True, stop=False, is_transpose=True)
+                    nc.tensor.matmul(block, m_t[b, jb][:, columns], identity[:], start=False, stop=True, is_transpose=True)
+                nc.scalar.copy(y[:, q0 * P : (q0 + per_bank) * P], sums[:])
             nc.vector.tensor_tensor(
-                pages[t][:].indirect(idx2[:, first * P // 16 : (first + count) * P // 16]),
+                page[:].indirect(idx2[:, first * P // PER_COLUMN : (first + count) * P // PER_COLUMN]),
                 y[:],
                 weights[t][:, first * P : (first + count) * P],
                 MULT,
             )
-            if first + count == blocks:
-                nc.sync.dma_start(out_rows[b, t], pages[t][:])
+            if first + count == BLOCKS:
+                nc.sync.dma_start(out_rows[b, t], page[:])
 
-        def place_all(b):
-            for pair in range(PACK // 2):
-                runs = [(0, 2), (2, 2), (4, 4)] if (b, pair) == (0, 0) else [(0, 4), (4, 4)]
-                for first, count in runs:
-                    for t in (2 * pair, 2 * pair + 1):
-                        place(b, t, first, count)
-
-        gate_rows(0, 0, 1)
-        table_planes()
-        constants()
-        table_words(0)
-        table_words(1)
-        weave_w1(0, 0)
-        quantize_w1(0, 0)
-        weave_w1(1, 0)
-        quantize_w1(1, 0)
-        weave_w1(0, 1)
-        quantize_w1(0, 1)
-        weave_w1(1, 1)
-        gate_rows(0, 1, 1)
-        quantize_w1(1, 1)
-        gate_rows(0, 2, 1)
-        gate_rows(0, 3, 1)
-        gate_rows(1, 0, 1)
-        gate_rows(1, 1, 1)
-        gate_rows(1, 2, 1)
-        gate_rows(1, 3, 2)
-        first_product(0)
-        first_product(1)
-        late_loads()
-        quantize_d(0, 0, 8, "B")
-        quantize_d(1, 0, 4, "A")
+        quantize_d(0, 0, BLOCKS, "then_d0")
+        quantize_d(1, 0, HALF_BLOCKS, "then_d1")
         second_product(0, 0)
-        quantize_d(1, 4, 4, "A")
+        quantize_d(1, HALF_BLOCKS, HALF_BLOCKS, "then_d1")
         second_product(0, 1)
-        place_all(0)
-        second_product(1, 0)
-        second_product(1, 1)
-        place_all(1)
+
+        quarter = BLOCKS // 4
+        for first, count in ((0, quarter), (quarter, quarter), (HALF_BLOCKS, HALF_BLOCKS)):
+            for b, t in row_tiles[:2]:
+                place(b, t, first, count)
+        for b, t in row_tiles[2:PACK]:
+            place(b, t, 0, BLOCKS)
+        for half in range(2):
+            second_product(1, half)
+        for b, t in row_tiles[PACK:]:
+            place(b, t, 0, BLOCKS)

@@ -33,7 +33,6 @@ ALIGN = 64
 RUN = 2
 PAGES = 3
 
-WINDOW_BUFS = 6
 ROW_BUFS = 5
 Y_BUFS = 3
 MX_BANKS, H_BANKS, Y_BANKS = 3, 3, 2
@@ -46,7 +45,6 @@ def tile_list_leak_residual_backward_kernel(
     with ExitStack() as ctx:
         lists = ctx.enter_context(tc.tile_pool(name="lists", bufs=1))
         keep = ctx.enter_context(tc.tile_pool(name="keep", bufs=1))
-        windows = ctx.enter_context(tc.tile_pool(name="windows", bufs=WINDOW_BUFS))
         rows = ctx.enter_context(tc.tile_pool(name="rows", bufs=ROW_BUFS))
         turns = ctx.enter_context(tc.tile_pool(name="turns", bufs=1))
         staged = ctx.enter_context(tc.tile_pool(name="staged", bufs=Y_BUFS))
@@ -84,13 +82,13 @@ def tile_list_leak_residual_backward_kernel(
                 nc.scalar.activation(gate, xs, IDENTITY, bias=slope[:, b, t : t + 1], scale=neg_slope[:, b, t : t + 1])
                 nc.gpsimd.tensor_tensor(gate, gate, xs, MULT)
 
-        def streamed_window():
-            return windows.tile([P, T], F32, name="s_window", tag="window", align_bytes=ALIGN)
+        def slot(name, shape, dtype, tenant):
+            return turns.tile(shape, dtype, name=tenant, tag=name, align_bytes=ALIGN)
 
-        def turn_window(turn):
-            return turns.tile([P, T], F32, name="s_window", tag=turn, align_bytes=ALIGN)
+        def s_window(i):
+            return slot("s%d" % i, [P, T], F32, "s_window")
 
-        make_gate(0, 0, streamed_window())
+        make_gate(0, 0, s_window(0))
 
         v_planes = [keep.tile([P, S], U8, name="v_plane%d" % a, align_bytes=ALIGN) for a in range(PASSES)]
         for q in range(QUADS):
@@ -111,14 +109,14 @@ def tile_list_leak_residual_backward_kernel(
 
         v_words = []
         for a in range(PASSES):
-            window = windows.tile([P, T], U32, name="tab_window", tag="window", align_bytes=ALIGN)
+            window = slot("tab%d" % a, [P, T], U32, "tab_window")
             nc.sync.dma_start(window[:].bitcast(I32), tab_words[a].rearrange("p c i -> p (c i)").bitcast(I32))
             words = keep.tile([P, S], U32, name="v_words%d" % a, align_bytes=ALIGN)
             nc.vector.tensor_copy(words[:], window[:].indirect(idx[:]))
             v_words.append(words)
 
         def weave_w1(a, b):
-            raw = windows.tile([P, PACK, BANK], F32, name="w1_raw", tag="window", align_bytes=ALIGN)
+            raw = slot("w1_%d%d" % (a, b), [P, PACK, BANK], F32, "w1_raw")
             nc.sync.dma_start(
                 raw[:],
                 w1[a * PASS : (a + 1) * PASS, b * BANK : (b + 1) * BANK].rearrange("(p t) c -> p t c", t=PACK),
@@ -143,14 +141,13 @@ def tile_list_leak_residual_backward_kernel(
             quantize_w1(a, b, woven, keep.tile([P, BANK], U32, name="w1_words%d%d" % (a, b), align_bytes=ALIGN))
         last_a, last_b = w1_pieces[-1]
         woven = weave_w1(last_a, last_b)
-        make_gate(0, 1, turn_window("then_w1"))
-        quantize_w1(last_a, last_b, woven, turns.tile([P, BANK], U32, name="w1_last", tag="then_w1", align_bytes=ALIGN))
+        make_gate(0, 1, s_window(1))
+        quantize_w1(last_a, last_b, woven, slot("s1", [P, BANK], U32, "w1_last"))
 
         row_tiles = [(b, t) for b in range(PASSES) for t in range(PACK)]
-        for b, t in row_tiles[2:-2]:
-            make_gate(b, t, streamed_window())
-        make_gate(*row_tiles[-2], turn_window("then_d1"))
-        make_gate(*row_tiles[-1], turn_window("then_d0"), pieces=2)
+        for i in range(2, len(row_tiles) - 1):
+            make_gate(*row_tiles[i], s_window(i))
+        make_gate(*row_tiles[-1], s_window(len(row_tiles) - 1), pieces=2)
 
         def product(lhs, rhs, dtype):
             acc = psum.tile([P, BANK], F32, name="acc", tag="mx", bufs=MX_BANKS)
@@ -170,21 +167,23 @@ def tile_list_leak_residual_backward_kernel(
             nc.scalar.copy(dst.rearrange("p (t m) -> p t m", t=PACK), acc[:].rearrange("p (m t) -> p t m", t=PACK))
 
         h_t = {}
-        for b in range(PASSES):
-            for jb in range(BLOCKS):
+        for b, half, name in ((0, 0, "tab0"), (0, 1, "tab1"), (1, 0, "w1_00"), (1, 1, "w1_10")):
+            copies = slot(name, [P, HALF_BLOCKS, BANK], F32, "h_t")
+            for jb in range(half * HALF_BLOCKS, (half + 1) * HALF_BLOCKS):
                 entries = slice(jb * P, (jb + 1) * P)
                 acc = product(
                     [(v_words[a][:, entries], v_planes[a][:, entries]) for a in range(PASSES)],
                     [(w1_mx[a, b][0][:], w1_mx[a, b][1][:]) for a in range(PASSES)],
                     E5M2,
                 )
-                h_t[b, jb] = keep.tile([P, BANK], F32, name="h_t%d%d" % (b, jb), align_bytes=ALIGN)
-                copy_by_row_tile(h_t[b, jb][:], acc)
+                h_t[b, jb] = copies[:, jb % HALF_BLOCKS, :]
+                copy_by_row_tile(h_t[b, jb], acc)
 
         w2_mx = []
+        w2_both = slot("w1_01", [P, PASSES * N], U32, "w2_both")
         for a in range(PASSES):
-            words = keep.tile([P, N], U32, name="w2_words%d" % a, align_bytes=ALIGN)
-            nc.sync.dma_start(words[:].bitcast(I32), w2_words[a].rearrange("p c i -> p (c i)").bitcast(I32))
+            words = w2_both[:, a * N : (a + 1) * N]
+            nc.sync.dma_start(words.bitcast(I32), w2_words[a].rearrange("p c i -> p (c i)").bitcast(I32))
             w2_mx.append((words, w2_planes[PLANE_ROWS * a : P, :]))
         for q in range(QUADS):
             nc.sync.dma_start(
@@ -195,7 +194,9 @@ def tile_list_leak_residual_backward_kernel(
         wgo_rows = wgo.rearrange("(m t) j -> t m j", t=PACK)
         weights = []
         for t in range(PACK):
-            weight = rows.tile([P, S], F32, name="weight", tag="row", align_bytes=ALIGN)
+            if t % 2 == 0:
+                pair = slot(("s0", "w1_11")[t // 2], [P, 2 * S], F32, "weight")
+            weight = pair[:, (t % 2) * S : (t % 2 + 1) * S]
             for q in range(QUADS):
                 nc.sync.dma_start(weight[QUAD * q : QUAD * (q + 1), :], wgo_rows[t])
             weights.append(weight)
@@ -223,10 +224,14 @@ def tile_list_leak_residual_backward_kernel(
 
         m_t = {}
 
-        def second_product(b, half):
+        m_tiles = {}
+
+        def second_product(b, half, blocks=range(HALF_BLOCKS)):
             columns = slice(b * BANK, (b + 1) * BANK)
-            copies = windows.tile([P, HALF_BLOCKS, BANK], F32, name="m_t", tag="window", align_bytes=ALIGN)
-            for q in range(HALF_BLOCKS):
+            if (b, half) not in m_tiles:
+                m_tiles[b, half] = slot("s%d" % (2 + 2 * b + half), [P, HALF_BLOCKS, BANK], F32, "m_t")
+            copies = m_tiles[b, half]
+            for q in blocks:
                 jb = half * HALF_BLOCKS + q
                 acc = product(
                     [d_mx[a, jb] for a in range(PASSES)],
@@ -258,14 +263,17 @@ def tile_list_leak_residual_backward_kernel(
             if first + count == BLOCKS:
                 nc.sync.dma_start(out_rows[b, t], page[:])
 
-        quantize_d(0, 0, BLOCKS, "then_d0")
-        quantize_d(1, 0, HALF_BLOCKS, "then_d1")
-        second_product(0, 0)
-        quantize_d(1, HALF_BLOCKS, HALF_BLOCKS, "then_d1")
-        second_product(0, 1)
-
+        quantize_d(0, 0, BLOCKS, "s7")
         quarter = BLOCKS // 4
+        quantize_d(1, 0, quarter, "s6")
+        second_product(0, 0, range(quarter))
+        quantize_d(1, quarter, quarter, "s1")
+        quantize_d(1, HALF_BLOCKS, HALF_BLOCKS, "s6")
         for first, count in ((0, quarter), (quarter, quarter), (HALF_BLOCKS, HALF_BLOCKS)):
+            if first == quarter:
+                second_product(0, 0, range(quarter, HALF_BLOCKS))
+            if first == HALF_BLOCKS:
+                second_product(0, 1)
             for b, t in row_tiles[:2]:
                 place(b, t, first, count)
         for b, t in row_tiles[2:PACK]:

@@ -31,6 +31,7 @@ HALF_BLOCKS = BLOCKS // 2
 PER_COLUMN = 16
 ALIGN = 64
 RUN = 2
+SCALAR_WEAVES = 3
 PAGES = 3
 
 ROW_BUFS = 5
@@ -115,14 +116,14 @@ def tile_list_leak_residual_backward_kernel(
             nc.vector.tensor_copy(words[:], window[:].indirect(idx[:]))
             v_words.append(words)
 
-        def weave_w1(a, b):
+        def weave_w1(a, b, copy):
             raw = slot("w1_%d%d" % (a, b), [P, PACK, BANK], F32, "w1_raw")
             nc.sync.dma_start(
                 raw[:],
                 w1[a * PASS : (a + 1) * PASS, b * BANK : (b + 1) * BANK].rearrange("(p t) c -> p t c", t=PACK),
             )
             woven = rows.tile([P, PACK * BANK], BF16, name="w1_woven", tag="row", align_bytes=ALIGN)
-            nc.scalar.copy(
+            copy(
                 woven[:].rearrange("p (c i t) -> p c t i", i=RUN, t=PACK),
                 raw[:].rearrange("p t (c i) -> p c t i", i=RUN),
             )
@@ -136,13 +137,10 @@ def tile_list_leak_residual_backward_kernel(
             w1_mx[a, b] = (words, plane)
 
         w1_pieces = [(a, b) for b in range(PASSES) for a in range(PASSES)]
-        for a, b in w1_pieces[:-1]:
-            woven = weave_w1(a, b)
+        for k, (a, b) in enumerate(w1_pieces):
+            woven = weave_w1(a, b, nc.scalar.copy if k < SCALAR_WEAVES else nc.vector.tensor_copy)
             quantize_w1(a, b, woven, keep.tile([P, BANK], U32, name="w1_words%d%d" % (a, b), align_bytes=ALIGN))
-        last_a, last_b = w1_pieces[-1]
-        woven = weave_w1(last_a, last_b)
         make_gate(0, 1, s_window(1))
-        quantize_w1(last_a, last_b, woven, slot("s1", [P, BANK], U32, "w1_last"))
 
         row_tiles = [(b, t) for b in range(PASSES) for t in range(PACK)]
         for i in range(2, len(row_tiles) - 1):

@@ -36,7 +36,7 @@ PAGES = 3
 
 ROW_BUFS = 5
 Y_BUFS = 3
-MX_BANKS, H_BANKS, Y_BANKS = 3, 3, 2
+MX_BANKS, ROW_BANKS = 2, 6
 
 
 def tile_list_leak_residual_backward_kernel(
@@ -205,7 +205,7 @@ def tile_list_leak_residual_backward_kernel(
             woven = turns.tile([P, count * BANK], BF16, name="d_woven", tag=turn, align_bytes=ALIGN)
             for q in range(count):
                 half, column = divmod((first + q) * P, HALF)
-                h_rows = psum.tile([P, PACK, P], F32, name="h_rows", tag="h", bufs=H_BANKS)
+                h_rows = psum.tile([P, PACK, P], F32, name="h_rows", tag="row", bufs=ROW_BANKS)
                 for t in range(PACK):
                     nc.tensor.transpose(h_rows[:, t, :], h_t[b, first + q][:, t * P : (t + 1) * P], identity[:])
                 nc.vector.tensor_tensor(
@@ -245,7 +245,7 @@ def tile_list_leak_residual_backward_kernel(
             y = staged.tile([P, count * P], F32, name="y", tag="y", align_bytes=ALIGN)
             per_bank = min(count, BANK // P)
             for q0 in range(0, count, per_bank):
-                sums = psum.tile([P, per_bank * P], F32, name="sums", tag="y", bufs=Y_BANKS)
+                sums = psum.tile([P, per_bank * P], F32, name="sums", tag="row", bufs=ROW_BANKS)
                 for q in range(per_bank):
                     jb = first + q0 + q
                     block = sums[:, q * P : (q + 1) * P]

@@ -92,10 +92,10 @@ def tile_list_leak_residual_backward_kernel(
         make_gate(0, 0, s_window(0))
 
         v_planes = [keep.tile([P, S], U8, name="v_plane%d" % a, align_bytes=ALIGN) for a in range(PASSES)]
-        for q in range(QUADS):
+        for r in range(PLANE_ROWS):
             nc.sync.dma_start(
-                tab_planes[QUAD * q : QUAD * q + PLANE_ROWS, :].bitcast(I32).rearrange("r (a w) -> r a w", a=PASSES),
-                tab_scales[:, PLANE_ROWS * q : PLANE_ROWS * (q + 1), :].bitcast(I32).rearrange("a r w -> r a w"),
+                tab_planes[r:P:QUAD, :].bitcast(I32).rearrange("q (a w) -> q a w", a=PASSES),
+                tab_scales[:, r : PLANE_ROWS * QUADS : PLANE_ROWS, :].bitcast(I32).rearrange("a q w -> q a w"),
             )
         for a in range(PASSES):
             nc.vector.tensor_copy(v_planes[a][:], tab_planes[:, a * T : (a + 1) * T].indirect(idx[:]))

@@ -31,7 +31,7 @@ HALF_BLOCKS = BLOCKS // 2
 PER_COLUMN = 16
 ALIGN = 64
 RUN = 2
-SCALAR_WEAVES = 3
+SCALAR_WEAVES = 2
 PAGES = 3
 
 ROW_BUFS = 5
@@ -56,7 +56,7 @@ def tile_list_leak_residual_backward_kernel(
         s_rows = sT.rearrange("(b p t) c -> b t p c", b=PASSES, t=PACK)
         out_rows = out.rearrange("(b p t) c -> b t p c", b=PASSES, t=PACK)
 
-        tab_planes = keep.tile([P, PASSES * T], U8, name="tab_planes", align_bytes=ALIGN)
+        tab_planes = turns.tile([P, T], U8, name="tab_planes", tag="first", align_bytes=ALIGN)
         nc.gpsimd.memset(tab_planes[:].bitcast(I32), 0)
         nc.sync.dma_start(idx[:], offs)
 
@@ -67,9 +67,10 @@ def tile_list_leak_residual_backward_kernel(
 
         gates = [keep.tile([P, 2, PACK, HALF], F32, name="gate%d" % b, align_bytes=ALIGN) for b in range(PASSES)]
 
-        def make_gate(b, t, window, pieces=1):
-            nc.sync.dma_start(window[:], s_rows[b, t])
-            x = rows.tile([P, 2, HALF], F32, name="x", tag="row", align_bytes=ALIGN)
+        def make_gate(b, t, window, pieces=1, x=None):
+            if x is None:
+                nc.sync.dma_start(window[:], s_rows[b, t])
+                x = rows.tile([P, 2, HALF], F32, name="x", tag="row", align_bytes=ALIGN)
             halves = 2 // pieces
             columns = S // PER_COLUMN // pieces
             for c in range(pieces):
@@ -89,16 +90,21 @@ def tile_list_leak_residual_backward_kernel(
         def s_window(i):
             return slot("s%d" % i, [P, T], F32, "s_window")
 
-        make_gate(0, 0, s_window(0))
+        first_window = s_window(0)
+        nc.sync.dma_start(first_window[:], s_rows[0, 0])
 
         v_planes = [keep.tile([P, S], U8, name="v_plane%d" % a, align_bytes=ALIGN) for a in range(PASSES)]
+        nc.gpsimd.memset(v_planes[1][:].bitcast(I32), 0)
+        scale_rows = tab_scales.bitcast(I32).rearrange("a (q r) w -> r q a w", r=PLANE_ROWS)
         for r in range(PLANE_ROWS):
-            nc.sync.dma_start(
-                tab_planes[r:P:QUAD, :].bitcast(I32).rearrange("q (a w) -> q a w", a=PASSES),
-                tab_scales[:, r : PLANE_ROWS * QUADS : PLANE_ROWS, :].bitcast(I32).rearrange("a q w -> q a w"),
+            nc.sync.dma_start(tab_planes[r : P : QUAD // PASSES, :].bitcast(I32), scale_rows[r])
+        nc.vector.tensor_copy(v_planes[0][:], tab_planes[:].indirect(idx[:]))
+        for r in range(PLANE_ROWS):
+            nc.scalar.dma_start(
+                v_planes[1][r:P:QUAD, :].bitcast(I32),
+                v_planes[0][QUAD // PASSES + r : P : QUAD, :].bitcast(I32),
             )
-        for a in range(PASSES):
-            nc.vector.tensor_copy(v_planes[a][:], tab_planes[:, a * T : (a + 1) * T].indirect(idx[:]))
+        make_gate(0, 0, first_window, x=slot("first", [P, 2, HALF], F32, "x"))
 
         identity = keep.tile([P, P], F32, name="identity")
         make_identity(nc, identity[:])

@@ -65,9 +65,9 @@ def tile_list_leak_residual_backward_kernel(
         nc.scalar.dma_start(slope[:], beta.rearrange("(b p t) -> p b t", b=PASSES, t=PACK))
         nc.scalar.activation(neg_slope[:], slope[:], IDENTITY, scale=-1.0)
 
-        gates = [keep.tile([P, 2, PACK, HALF], F32, name="gate%d" % b, align_bytes=ALIGN) for b in range(PASSES)]
+        gates = {}
 
-        def make_gate(b, t, window, pieces=1, x=None):
+        def make_gate(b, t, window, pieces=1, x=None, later=False):
             if x is None:
                 nc.sync.dma_start(window[:], s_rows[b, t])
                 x = rows.tile([P, 2, HALF], F32, name="x", tag="row", align_bytes=ALIGN)
@@ -78,8 +78,16 @@ def tile_list_leak_residual_backward_kernel(
                     x[:, c * halves : (c + 1) * halves, :].rearrange("p h j -> p (h j)"),
                     window[:].indirect(idx[:, c * columns : (c + 1) * columns]),
                 )
+            if later:
+                return x
+            finish_gate(b, t, x, pieces)
+
+        def finish_gate(b, t, x, pieces=1):
+            halves = 2 // pieces
             for c in range(pieces):
                 xs = x[:, c * halves : (c + 1) * halves, :]
+                if b not in gates:
+                    gates[b] = slot("gate%d" % b, [P, 2, PACK, HALF], F32, "gate")
                 gate = gates[b][:, c * halves : (c + 1) * halves, t, :]
                 nc.scalar.activation(gate, xs, IDENTITY, bias=slope[:, b, t : t + 1], scale=neg_slope[:, b, t : t + 1])
                 nc.gpsimd.tensor_tensor(gate, gate, xs, MULT)
@@ -104,7 +112,7 @@ def tile_list_leak_residual_backward_kernel(
                 v_planes[1][r:P:QUAD, :].bitcast(I32),
                 v_planes[0][QUAD // PASSES + r : P : QUAD, :].bitcast(I32),
             )
-        make_gate(0, 0, first_window, x=slot("first", [P, 2, HALF], F32, "x"))
+        first_x = make_gate(0, 0, first_window, x=slot("first", [P, 2, HALF], F32, "x"), later=True)
 
         identity = keep.tile([P, P], F32, name="identity")
         make_identity(nc, identity[:])
@@ -128,7 +136,10 @@ def tile_list_leak_residual_backward_kernel(
                 raw[:],
                 w1[a * PASS : (a + 1) * PASS, b * BANK : (b + 1) * BANK].rearrange("(p t) c -> p t c", t=PACK),
             )
-            woven = rows.tile([P, PACK * BANK], BF16, name="w1_woven", tag="row", align_bytes=ALIGN)
+            if (a, b) == (PASSES - 1, PASSES - 1):
+                woven = slot("gate0", [P, PACK * BANK], BF16, "w1_woven")
+            else:
+                woven = rows.tile([P, PACK * BANK], BF16, name="w1_woven", tag="row", align_bytes=ALIGN)
             copy(
                 woven[:].rearrange("p (c i t) -> p c t i", i=RUN, t=PACK),
                 raw[:].rearrange("p t (c i) -> p c t i", i=RUN),
@@ -146,6 +157,7 @@ def tile_list_leak_residual_backward_kernel(
         for k, (a, b) in enumerate(w1_pieces):
             woven = weave_w1(a, b, nc.scalar.copy if k < SCALAR_WEAVES else nc.vector.tensor_copy)
             quantize_w1(a, b, woven, keep.tile([P, BANK], U32, name="w1_words%d%d" % (a, b), align_bytes=ALIGN))
+        finish_gate(0, 0, first_x)
         make_gate(0, 1, s_window(1))
 
         row_tiles = [(b, t) for b in range(PASSES) for t in range(PACK)]
@@ -270,8 +282,8 @@ def tile_list_leak_residual_backward_kernel(
         quantize_d(0, 0, BLOCKS, "s7")
         quarter = BLOCKS // 4
         quantize_d(1, 0, quarter, "s6")
-        second_product(0, 0, range(quarter))
         quantize_d(1, quarter, quarter, "s1")
+        second_product(0, 0, range(quarter))
         quantize_d(1, HALF_BLOCKS, HALF_BLOCKS, "s6")
         for first, count in ((0, quarter), (quarter, quarter), (HALF_BLOCKS, HALF_BLOCKS)):
             if first == quarter:

@@ -92,6 +92,11 @@ def tile_list_leak_residual_backward_kernel(
                 nc.scalar.activation(gate, xs, IDENTITY, bias=slope[:, b, t : t + 1], scale=neg_slope[:, b, t : t + 1])
                 nc.gpsimd.tensor_tensor(gate, gate, xs, MULT)
 
+        def half_gate(b, t, half, xs):
+            gate = gates[b][:, half, t, :]
+            nc.scalar.activation(gate, xs, IDENTITY, bias=slope[:, b, t : t + 1], scale=neg_slope[:, b, t : t + 1])
+            nc.gpsimd.tensor_tensor(gate, gate, xs, MULT)
+
         def slot(name, shape, dtype, tenant):
             return turns.tile(shape, dtype, name=tenant, tag=name, align_bytes=ALIGN)
 
@@ -161,9 +166,20 @@ def tile_list_leak_residual_backward_kernel(
         make_gate(0, 1, s_window(1))
 
         row_tiles = [(b, t) for b in range(PASSES) for t in range(PACK)]
-        for i in range(2, len(row_tiles) - 1):
+        for i in range(2, len(row_tiles) - 2):
             make_gate(*row_tiles[i], s_window(i))
-        make_gate(*row_tiles[-1], s_window(len(row_tiles) - 1), pieces=2)
+        b = PASSES - 1
+        seventh_x = make_gate(b, PACK - 2, s_window(len(row_tiles) - 2), later=True)
+        half_gate(b, PACK - 2, 0, seventh_x[:, 0, :])
+        last_window = s_window(len(row_tiles) - 1)
+        nc.sync.dma_start(last_window[:], s_rows[b, PACK - 1])
+        last_x = [gates[b][:, 1, PACK - 2, :], rows.tile([P, HALF], F32, name="x", tag="row", align_bytes=ALIGN)[:]]
+        for half in range(2):
+            columns = S // PER_COLUMN // 2
+            nc.vector.tensor_copy(last_x[half], last_window[:].indirect(idx[:, half * columns : (half + 1) * columns]))
+        half_gate(b, PACK - 1, 0, last_x[0])
+        half_gate(b, PACK - 2, 1, seventh_x[:, 1, :])
+        half_gate(b, PACK - 1, 1, last_x[1])
 
         def product(lhs, rhs, dtype):
             acc = psum.tile([P, BANK], F32, name="acc", tag="mx", bufs=MX_BANKS)

@@ -235,7 +235,7 @@ def tile_list_leak_residual_backward_kernel(
 
         d_mx = {}
 
-        def quantize_d(b, first, count, turn):
+        def weave_d(b, first, count, turn):
             woven = turns.tile([P, count * BANK], BF16, name="d_woven", tag=turn, align_bytes=ALIGN)
             for q in range(count):
                 half, column = divmod((first + q) * P, HALF)
@@ -248,6 +248,12 @@ def tile_list_leak_residual_backward_kernel(
                     gates[b][:, half, :, column : column + P].rearrange("p t (c i) -> p c t i", i=RUN),
                     MULT,
                 )
+            return woven
+
+        def quantize_d(b, first, count, turn):
+            quantize_woven(b, first, count, weave_d(b, first, count, turn))
+
+        def quantize_woven(b, first, count, woven):
             words = keep.tile([P, count * P], U32, name="d_words%d%d" % (b, first), align_bytes=ALIGN)
             plane = keep.tile([P, count * P], U8, name="d_plane%d%d" % (b, first), align_bytes=ALIGN)
             nc.vector.quantize_mx(words[:].bitcast(E4M3), plane[:], woven[:])
@@ -295,9 +301,10 @@ def tile_list_leak_residual_backward_kernel(
             if first + count == BLOCKS:
                 nc.sync.dma_start(out_rows[b, t], page[:])
 
-        quantize_d(0, 0, BLOCKS, "s7")
         quarter = BLOCKS // 4
-        quantize_d(1, 0, quarter, "s6")
+        woven = [weave_d(0, 0, BLOCKS, "s7"), weave_d(1, 0, quarter, "s6")]
+        quantize_woven(0, 0, BLOCKS, woven[0])
+        quantize_woven(1, 0, quarter, woven[1])
         quantize_d(1, quarter, quarter, "s1")
         second_product(0, 0, range(quarter))
         quantize_d(1, HALF_BLOCKS, HALF_BLOCKS, "s6")

@@ -58,7 +58,6 @@ def tile_list_leak_residual_backward_kernel(
 
         tab_planes = turns.tile([P, T], U8, name="tab_planes", tag="first", align_bytes=ALIGN)
         nc.gpsimd.memset(tab_planes[:].bitcast(I32), 0)
-        nc.sync.dma_start(idx[:], offs)
 
         slope = keep.tile([P, PASSES, PACK], F32, name="slope")
         neg_slope = keep.tile([P, PASSES, PACK], F32, name="neg_slope")
@@ -105,6 +104,7 @@ def tile_list_leak_residual_backward_kernel(
 
         first_window = s_window(0)
         nc.sync.dma_start(first_window[:], s_rows[0, 0])
+        nc.sync.dma_start(idx[:], offs)
 
         v_planes = [keep.tile([P, S], U8, name="v_plane%d" % a, align_bytes=ALIGN) for a in range(PASSES)]
         nc.gpsimd.memset(v_planes[1][:].bitcast(I32), 0)
@@ -286,11 +286,16 @@ def tile_list_leak_residual_backward_kernel(
             per_bank = min(count, BANK // P)
             for q0 in range(0, count, per_bank):
                 sums = psum.tile([P, per_bank * P], F32, name="sums", tag="row", bufs=ROW_BANKS)
-                for q in range(per_bank):
-                    jb = first + q0 + q
-                    block = sums[:, q * P : (q + 1) * P]
-                    nc.tensor.matmul(block, h_t[b, jb][:, columns], identity[:], start=True, stop=False, is_transpose=True)
-                    nc.tensor.matmul(block, m_t[b, jb][:, columns], identity[:], start=False, stop=True, is_transpose=True)
+                for k, part in enumerate((h_t, m_t)):
+                    for q in range(per_bank):
+                        nc.tensor.matmul(
+                            sums[:, q * P : (q + 1) * P],
+                            part[b, first + q0 + q][:, columns],
+                            identity[:],
+                            start=(k == 0 and q == 0),
+                            stop=(k == 1 and q == per_bank - 1),
+                            is_transpose=True,
+                        )
                 nc.scalar.copy(y[:, q0 * P : (q0 + per_bank) * P], sums[:])
             nc.vector.tensor_tensor(
                 page[:].indirect(idx2[:, first * P // PER_COLUMN : (first + count) * P // PER_COLUMN]),

@@ -59,10 +59,11 @@ def tile_list_leak_residual_backward_kernel(
         tab_planes = turns.tile([P, T], U8, name="tab_planes", tag="first", align_bytes=ALIGN)
         nc.gpsimd.memset(tab_planes[:].bitcast(I32), 0)
 
-        slope = keep.tile([P, PASSES, PACK], F32, name="slope")
-        neg_slope = keep.tile([P, PASSES, PACK], F32, name="neg_slope")
-        nc.scalar.dma_start(slope[:], beta.rearrange("(b p t) -> p b t", b=PASSES, t=PACK))
-        nc.scalar.activation(neg_slope[:], slope[:], IDENTITY, scale=-1.0)
+        slope = keep.tile([P, PACK, PASSES], F32, name="slope")
+        neg_slope = keep.tile([P, PACK, PASSES], F32, name="neg_slope")
+        beta_rows = keep.tile([P, PASS], F32, name="beta_rows")
+        nc.gpsimd.memset(beta_rows[:], 0.0)
+        nc.scalar.dma_start(beta_rows[0:PASSES, :], beta.rearrange("(b r) -> b r", b=PASSES))
 
         gates = {}
 
@@ -88,12 +89,12 @@ def tile_list_leak_residual_backward_kernel(
                 if b not in gates:
                     gates[b] = slot("gate%d" % b, [P, 2, PACK, HALF], F32, "gate")
                 gate = gates[b][:, c * halves : (c + 1) * halves, t, :]
-                nc.scalar.activation(gate, xs, IDENTITY, bias=slope[:, b, t : t + 1], scale=neg_slope[:, b, t : t + 1])
+                nc.scalar.activation(gate, xs, IDENTITY, bias=slope[:, t, b : b + 1], scale=neg_slope[:, t, b : b + 1])
                 nc.gpsimd.tensor_tensor(gate, gate, xs, MULT)
 
         def half_gate(b, t, half, xs):
             gate = gates[b][:, half, t, :]
-            nc.scalar.activation(gate, xs, IDENTITY, bias=slope[:, b, t : t + 1], scale=neg_slope[:, b, t : t + 1])
+            nc.scalar.activation(gate, xs, IDENTITY, bias=slope[:, t, b : b + 1], scale=neg_slope[:, t, b : b + 1])
             nc.gpsimd.tensor_tensor(gate, gate, xs, MULT)
 
         def slot(name, shape, dtype, tenant):
@@ -121,6 +122,11 @@ def tile_list_leak_residual_backward_kernel(
 
         identity = keep.tile([P, P], F32, name="identity")
         make_identity(nc, identity[:])
+        turned = psum.tile([P, PACK, P], F32, name="turned", tag="mx", bufs=MX_BANKS)
+        for t in range(PACK):
+            nc.tensor.transpose(turned[:, t, :], beta_rows[:, t:PASS:PACK], identity[:])
+        nc.scalar.activation(slope[:], turned[:, :, 0:PASSES], IDENTITY)
+        nc.scalar.activation(neg_slope[:], turned[:, :, 0:PASSES], IDENTITY, scale=-1.0)
         w2_planes = keep.tile([P, N], U8, name="w2_planes", align_bytes=ALIGN)
         nc.gpsimd.memset(w2_planes[:].bitcast(I32), 0)
         pages = [keep.tile([P, T2], F32, name="page%d" % i, align_bytes=ALIGN) for i in range(PAGES)]

@@ -187,8 +187,8 @@ def tile_list_leak_residual_backward_kernel(
         half_gate(b, PACK - 2, 1, seventh_x[:, 1, :])
         half_gate(b, PACK - 1, 1, last_x[1])
 
-        def product(lhs, rhs, dtype):
-            acc = psum.tile([P, BANK], F32, name="acc", tag="mx", bufs=MX_BANKS)
+        def product(lhs, rhs, dtype, tag="mx", bufs=MX_BANKS):
+            acc = psum.tile([P, BANK], F32, name="acc", tag=tag, bufs=bufs)
             for a in range(PASSES):
                 nc.tensor.matmul_mx(
                     acc[:],
@@ -281,6 +281,7 @@ def tile_list_leak_residual_backward_kernel(
                     [d_mx[a, jb] for a in range(PASSES)],
                     [(w2_mx[a][0][:, columns], w2_mx[a][1][:, columns]) for a in range(PASSES)],
                     E4M3,
+                    *(("row", ROW_BANKS) if (b, half) == (0, 1) and q % 2 else ()),
                 )
                 m_t[b, jb] = copies[:, q, :]
                 copy_by_row_tile(m_t[b, jb], acc)

from contextlib import ExitStack

import concourse.mybir as mybir
from concourse.masks import make_identity

K, H, N, T, S, T2 = 1024, 1024, 1024, 2048, 1024, 2048
FLOPS = 2 * K * H * S + 2 * H * N * S

F32 = mybir.dt.float32
BF16 = mybir.dt.bfloat16
I32 = mybir.dt.int32
U32 = mybir.dt.uint32
U16 = mybir.dt.uint16
U8 = mybir.dt.uint8
E4M3 = mybir.dt.float8_e4m3fn_x4
E5M2 = mybir.dt.float8_e5m2_x4
MULT = mybir.AluOpType.mult
IDENTITY = mybir.ActivationFunctionType.Identity

P = 128
PACK = 4
PASS = P * PACK
PASSES = K // PASS
BANK = 512
QUAD = 32
QUADS = P // QUAD
PLANE_ROWS = 4
BLOCKS = S // P
HALF = S // 2
HALF_BLOCKS = BLOCKS // 2
PER_COLUMN = 16
ALIGN = 64
RUN = 2
SCALAR_WEAVES = 2
PAGES = 3

ROW_BUFS = 5
Y_BUFS = 3
MX_BANKS, ROW_BANKS = 2, 6


def tile_list_leak_residual_backward_kernel(
    tc, tab_words, tab_scales, offs, offs2, sT, w1, w2_words, w2_scales, beta, wgo, out
):
    nc = tc.nc
    with ExitStack() as ctx:
        lists = ctx.enter_context(tc.tile_pool(name="lists", bufs=1))
        keep = ctx.enter_context(tc.tile_pool(name="keep", bufs=1))
        rows = ctx.enter_context(tc.tile_pool(name="rows", bufs=ROW_BUFS))
        turns = ctx.enter_context(tc.tile_pool(name="turns", bufs=1))
        staged = ctx.enter_context(tc.tile_pool(name="staged", bufs=Y_BUFS))
        psum = ctx.enter_context(tc.psum_pool(name="psum", bufs=1))

        idx = lists.tile([P, S // PER_COLUMN], U16, name="idx")
        idx2 = lists.tile([P, S // PER_COLUMN], U16, name="idx2")
        s_rows = sT.rearrange("(b p t) c -> b t p c", b=PASSES, t=PACK)
        out_rows = out.rearrange("(b p t) c -> b t p c", b=PASSES, t=PACK)

        tab_planes = turns.tile([P, T], U8, name="tab_planes", tag="first", align_bytes=ALIGN)
        nc.gpsimd.memset(tab_planes[:].bitcast(I32), 0)

        slope = keep.tile([P, PACK, PASSES], F32, name="slope")
        neg_slope = keep.tile([P, PACK, PASSES], F32, name="neg_slope")
        beta_rows = keep.tile([P, PASS], F32, name="beta_rows")
        nc.gpsimd.memset(beta_rows[:], 0.0)
        nc.scalar.dma_start(beta_rows[0:PASSES, :], beta.rearrange("(b r) -> b r", b=PASSES))

        gates = {}

        def make_gate(b, t, window, pieces=1, x=None, later=False):
            if x is None:
                nc.sync.dma_start(window[:], s_rows[b, t])
                x = rows.tile([P, 2, HALF], F32, name="x", tag="row", align_bytes=ALIGN)
            halves = 2 // pieces
            columns = S // PER_COLUMN // pieces
            for c in range(pieces):
                nc.vector.tensor_copy(
                    x[:, c * halves : (c + 1) * halves, :].rearrange("p h j -> p (h j)"),
                    window[:].indirect(idx[:, c * columns : (c + 1) * columns]),
                )
            if later:
                return x
            finish_gate(b, t, x, pieces)

        def finish_gate(b, t, x, pieces=1):
            halves = 2 // pieces
            for c in range(pieces):
                xs = x[:, c * halves : (c + 1) * halves, :]
                if b not in gates:
                    gates[b] = slot("gate%d" % b, [P, 2, PACK, HALF], F32, "gate")
                gate = gates[b][:, c * halves : (c + 1) * halves, t, :]
                nc.scalar.activation(gate, xs, IDENTITY, bias=slope[:, t, b : b + 1], scale=neg_slope[:, t, b : b + 1])
                nc.gpsimd.tensor_tensor(gate, gate, xs, MULT)

        def half_gate(b, t, half, xs):
            gate = gates[b][:, half, t, :]
            nc.scalar.activation(gate, xs, IDENTITY, bias=slope[:, t, b : b + 1], scale=neg_slope[:, t, b : b + 1])
            nc.gpsimd.tensor_tensor(gate, gate, xs, MULT)

        def slot(name, shape, dtype, tenant):
            return turns.tile(shape, dtype, name=tenant, tag=name, align_bytes=ALIGN)

        def s_window(i):
            return slot("s%d" % i, [P, T], F32, "s_window")

        first_window = s_window(0)
        nc.sync.dma_start(first_window[:], s_rows[0, 0])
        nc.sync.dma_start(idx[:], offs)

        v_planes = [keep.tile([P, S], U8, name="v_plane%d" % a, align_bytes=ALIGN) for a in range(PASSES)]
        nc.gpsimd.memset(v_planes[1][:].bitcast(I32), 0)
        scale_rows = tab_scales.bitcast(I32).rearrange("a (q r) w -> r q a w", r=PLANE_ROWS)
        for r in range(PLANE_ROWS):
            nc.sync.dma_start(tab_planes[r : P : QUAD // PASSES, :].bitcast(I32), scale_rows[r])
        nc.vector.tensor_copy(v_planes[0][:], tab_planes[:].indirect(idx[:]))
        for r in range(PLANE_ROWS):
            nc.scalar.dma_start(
                v_planes[1][r:P:QUAD, :].bitcast(I32),
                v_planes[0][QUAD // PASSES + r : P : QUAD, :].bitcast(I32),
            )
        first_x = make_gate(0, 0, first_window, x=slot("first", [P, 2, HALF], F32, "x"), later=True)

        identity = keep.tile([P, P], F32, name="identity")
        make_identity(nc, identity[:])
        turned = psum.tile([P, PACK, P], F32, name="turned", tag="mx", bufs=MX_BANKS)
        for t in range(PACK):
            nc.tensor.transpose(turned[:, t, :], beta_rows[:, t:PASS:PACK], identity[:])
        nc.scalar.activation(slope[:], turned[:, :, 0:PASSES], IDENTITY)
        nc.scalar.activation(neg_slope[:], turned[:, :, 0:PASSES], IDENTITY, scale=-1.0)
        w2_planes = keep.tile([P, N], U8, name="w2_planes", align_bytes=ALIGN)
        nc.gpsimd.memset(w2_planes[:].bitcast(I32), 0)
        pages = [keep.tile([P, T2], F32, name="page%d" % i, align_bytes=ALIGN) for i in range(PAGES)]
        for page in pages:
            nc.gpsimd.memset(page[:], 0.0)

        v_words = []
        for a in range(PASSES):
            window = slot("tab%d" % a, [P, T], U32, "tab_window")
            nc.sync.dma_start(window[:].bitcast(I32), tab_words[a].rearrange("p c i -> p (c i)").bitcast(I32))
            words = keep.tile([P, S], U32, name="v_words%d" % a, align_bytes=ALIGN)
            nc.vector.tensor_copy(words[:], window[:].indirect(idx[:]))
            v_words.append(words)

        def weave_w1(a, b, copy):
            raw = slot("w1_%d%d" % (a, b), [P, PACK, BANK], F32, "w1_raw")
            nc.sync.dma_start(
                raw[:],
                w1[a * PASS : (a + 1) * PASS, b * BANK : (b + 1) * BANK].rearrange("(p t) c -> p t c", t=PACK),
            )
            if (a, b) == (PASSES - 1, PASSES - 1):
                woven = slot("gate0", [P, PACK * BANK], BF16, "w1_woven")
            else:
                woven = rows.tile([P, PACK * BANK], BF16, name="w1_woven", tag="row", align_bytes=ALIGN)
            copy(
                woven[:].rearrange("p (c i t) -> p c t i", i=RUN, t=PACK),
                raw[:].rearrange("p t (c i) -> p c t i", i=RUN),
            )
            return woven

        w1_mx = {}

        def quantize_w1(a, b, woven, words):
            plane = keep.tile([P, BANK], U8, name="w1_plane%d%d" % (a, b), align_bytes=ALIGN)
            nc.vector.quantize_mx(words[:].bitcast(E4M3), plane[:], woven[:])
            w1_mx[a, b] = (words, plane)

        w1_pieces = [(a, b) for b in range(PASSES) for a in range(PASSES)]
        for k, (a, b) in enumerate(w1_pieces):
            woven = weave_w1(a, b, nc.scalar.copy if k < SCALAR_WEAVES else nc.vector.tensor_copy)
            quantize_w1(a, b, woven, keep.tile([P, BANK], U32, name="w1_words%d%d" % (a, b), align_bytes=ALIGN))
        finish_gate(0, 0, first_x)
        make_gate(0, 1, s_window(1))

        row_tiles = [(b, t) for b in range(PASSES) for t in range(PACK)]
        for i in range(2, len(row_tiles) - 2):
            make_gate(*row_tiles[i], s_window(i))
        b = PASSES - 1
        seventh_x = make_gate(b, PACK - 2, s_window(len(row_tiles) - 2), later=True)
        half_gate(b, PACK - 2, 0, seventh_x[:, 0, :])
        last_window = s_window(len(row_tiles) - 1)
        nc.sync.dma_start(last_window[:], s_rows[b, PACK - 1])
        last_x = [gates[b][:, 1, PACK - 2, :], rows.tile([P, HALF], F32, name="x", tag="row", align_bytes=ALIGN)[:]]
        for half in range(2):
            columns = S // PER_COLUMN // 2
            nc.vector.tensor_copy(last_x[half], last_window[:].indirect(idx[:, half * columns : (half + 1) * columns]))
        half_gate(b, PACK - 1, 0, last_x[0])
        half_gate(b, PACK - 2, 1, seventh_x[:, 1, :])
        half_gate(b, PACK - 1, 1, last_x[1])

        def product(lhs, rhs, dtype, tag="mx", bufs=MX_BANKS):
            acc = psum.tile([P, BANK], F32, name="acc", tag=tag, bufs=bufs)
            for a in range(PASSES):
                nc.tensor.matmul_mx(
                    acc[:],
                    lhsT=lhs[a][0].bitcast(dtype),
                    lhsT_scale=lhs[a][1],
                    rhs=rhs[a][0].bitcast(E4M3),
                    rhs_scale=rhs[a][1],
                    start=(a == 0),
                    stop=(a == PASSES - 1),
                )
            return acc

        def copy_by_row_tile(dst, acc):
            nc.scalar.copy(dst.rearrange("p (t m) -> p t m", t=PACK), acc[:].rearrange("p (m t) -> p t m", t=PACK))

        h_t = {}
        for b, half, name in ((0, 0, "tab0"), (0, 1, "tab1"), (1, 0, "w1_00"), (1, 1, "w1_10")):
            copies = slot(name, [P, HALF_BLOCKS, BANK], F32, "h_t")
            for jb in range(half * HALF_BLOCKS, (half + 1) * HALF_BLOCKS):
                entries = slice(jb * P, (jb + 1) * P)
                acc = product(
                    [(v_words[a][:, entries], v_planes[a][:, entries]) for a in range(PASSES)],
                    [(w1_mx[a, b][0][:], w1_mx[a, b][1][:]) for a in range(PASSES)],
                    E5M2,
                )
                h_t[b, jb] = copies[:, jb % HALF_BLOCKS, :]
                copy_by_row_tile(h_t[b, jb], acc)

        w2_mx = []
        w2_both = slot("w1_01", [P, PASSES * N], U32, "w2_both")
        for a in range(PASSES):
            words = w2_both[:, a * N : (a + 1) * N]
            nc.sync.dma_start(words.bitcast(I32), w2_words[a].rearrange("p c i -> p (c i)").bitcast(I32))
            w2_mx.append((words, w2_planes[PLANE_ROWS * a : P, :]))
        for q in range(QUADS):
            nc.sync.dma_start(
                w2_planes[QUAD * q : QUAD * q + PLANE_ROWS * PASSES, :].bitcast(I32),
                w2_scales[:, PLANE_ROWS * q : PLANE_ROWS * (q + 1), :].bitcast(I32),
            )
        nc.sync.dma_start(idx2[:], offs2)
        wgo_rows = wgo.rearrange("(m t) j -> t m j", t=PACK)
        weights = []
        for t in range(PACK):
            if t % 2 == 0:
                pair = slot(("s0", "w1_11")[t // 2], [P, 2 * S], F32, "weight")
            weight = pair[:, (t % 2) * S : (t % 2 + 1) * S]
            for q in range(QUADS):
                nc.sync.dma_start(weight[QUAD * q : QUAD * (q + 1), :], wgo_rows[t])
            weights.append(weight)

        d_mx = {}

        def weave_d(b, first, count, turn):
            woven = turns.tile([P, count * BANK], BF16, name="d_woven", tag=turn, align_bytes=ALIGN)
            for q in range(count):
                half, column = divmod((first + q) * P, HALF)
                h_rows = psum.tile([P, PACK, P], F32, name="h_rows", tag="row", bufs=ROW_BANKS)
                for t in range(PACK):
                    nc.tensor.transpose(h_rows[:, t, :], h_t[b, first + q][:, t * P : (t + 1) * P], identity[:])
                nc.vector.tensor_tensor(
                    woven[:, q * BANK : (q + 1) * BANK].rearrange("p (c i t) -> p c t i", i=RUN, t=PACK),
                    h_rows[:].rearrange("p t (c i) -> p c t i", i=RUN),
                    gates[b][:, half, :, column : column + P].rearrange("p t (c i) -> p c t i", i=RUN),
                    MULT,
                )
            return woven

        def quantize_d(b, first, count, turn):
            quantize_woven(b, first, count, weave_d(b, first, count, turn))

        def quantize_woven(b, first, count, woven):
            words = keep.tile([P, count * P], U32, name="d_words%d%d" % (b, first), align_bytes=ALIGN)
            plane = keep.tile([P, count * P], U8, name="d_plane%d%d" % (b, first), align_bytes=ALIGN)
            nc.vector.quantize_mx(words[:].bitcast(E4M3), plane[:], woven[:])
            for q in range(count):
                d_mx[b, first + q] = (words[:, q * P : (q + 1) * P], plane[:, q * P : (q + 1) * P])

        m_t = {}

        m_tiles = {}

        def second_product(b, half, blocks=range(HALF_BLOCKS)):
            columns = slice(b * BANK, (b + 1) * BANK)
            if (b, half) not in m_tiles:
                m_tiles[b, half] = slot("s%d" % (2 + 2 * b + half), [P, HALF_BLOCKS, BANK], F32, "m_t")
            copies = m_tiles[b, half]
            for q in blocks:
                jb = half * HALF_BLOCKS + q
                acc = product(
                    [d_mx[a, jb] for a in range(PASSES)],
                    [(w2_mx[a][0][:, columns], w2_mx[a][1][:, columns]) for a in range(PASSES)],
                    E4M3,
                    *(("row", ROW_BANKS) if (b, half) == (0, 1) and q % 2 else ()),
                )
                m_t[b, jb] = copies[:, q, :]
                copy_by_row_tile(m_t[b, jb], acc)

        def place(b, t, first, count):
            page = pages[(PACK * b + t) % PAGES]
            columns = slice(t * P, (t + 1) * P)
            y = staged.tile([P, count * P], F32, name="y", tag="y", align_bytes=ALIGN)
            per_bank = min(count, BANK // P)
            for q0 in range(0, count, per_bank):
                sums = psum.tile([P, per_bank * P], F32, name="sums", tag="row", bufs=ROW_BANKS)
                for k, part in enumerate((h_t, m_t)):
                    for q in range(per_bank):
                        nc.tensor.matmul(
                            sums[:, q * P : (q + 1) * P],
                            part[b, first + q0 + q][:, columns],
                            identity[:],
                            start=(k == 0 and q == 0),
                            stop=(k == 1 and q == per_bank - 1),
                            is_transpose=True,
                        )
                nc.scalar.copy(y[:, q0 * P : (q0 + per_bank) * P], sums[:])
            nc.vector.tensor_tensor(
                page[:].indirect(idx2[:, first * P // PER_COLUMN : (first + count) * P // PER_COLUMN]),
                y[:],
                weights[t][:, first * P : (first + count) * P],
                MULT,
            )
            if first + count == BLOCKS:
                nc.sync.dma_start(out_rows[b, t], page[:])

        quarter = BLOCKS // 4
        woven = [weave_d(0, 0, BLOCKS, "s7"), weave_d(1, 0, quarter, "s6")]
        quantize_woven(0, 0, BLOCKS, woven[0])
        quantize_woven(1, 0, quarter, woven[1])
        quantize_d(1, quarter, quarter, "s1")
        second_product(0, 0, range(quarter))
        quantize_d(1, HALF_BLOCKS, HALF_BLOCKS, "s6")
        for first, count in ((0, quarter), (quarter, quarter), (HALF_BLOCKS, HALF_BLOCKS)):
            if first == quarter:
                second_product(0, 0, range(quarter, HALF_BLOCKS))
            if first == HALF_BLOCKS:
                second_product(0, 1)
            for b, t in row_tiles[:2]:
                place(b, t, first, count)
        for b, t in row_tiles[2:PACK]:
            place(b, t, 0, BLOCKS)
        for half in range(2):
            second_product(1, half)
        for b, t in row_tiles[PACK:]:
            place(b, t, 0, BLOCKS)
